import numpy as np, ml_dtypes
CORES = [242,247,114,119]
N = 4
import mx_ref
BF = ml_dtypes.bfloat16
def entries(a):
    return np.ascontiguousarray(a.T).reshape(-1)
def table(e):
    return np.ascontiguousarray(np.reshape(e, (-1, 16)).T).astype(np.int32)
def cols(t, e):
    v = np.concatenate([t.reshape(128, -1, 4), np.zeros((128, 1, 4), BF)], axis=1)
    return np.ascontiguousarray(v[:, e]).reshape(128, -1)
def cut(t, i, w=512):
    return t[:, w * i:w * i + w]
def f(rng, *shape):
    return mx_ref.flush((rng.standard_normal(shape, dtype=np.float32) * np.exp2(rng.integers(-2, 3, shape[:-1] + (1,)))).astype(BF))
def wide(rng, *shape, cols=0):
    v = rng.standard_normal(shape, dtype=np.float32) * np.exp2(rng.integers(-12, 13, shape)).astype(np.float32)
    if cols: v *= np.repeat(np.exp2(rng.integers(-cols, cols + 1, shape[:-2] + (1, shape[-1] // 4))) * (rng.random(shape[:-2] + (1, shape[-1] // 4)) > 0.0625), 4, axis=-1).astype(np.float32)
    return mx_ref.flush(v.astype(BF))
T, O = 256, 2
def places(rng, dest):
    e = np.zeros((N, T), int)
    for d in range(N): e[dest == d] = d * T + rng.permutation(T)
    return np.stack([table(e[r]) for r in range(N)])
def relabel(rng):
    p = rng.permutation(N)
    if np.all((p - np.arange(N)) % N == p[0]): p[[0, 1]] = p[[1, 0]]
    return p
def setup_inputs(rng):
    e = rng.permutation(N * T).reshape(N, T)
    return {"x": f(rng, N, 128, 4 * T), "to": np.stack([table(e[r]) for r in range(N)]), "w": f(rng, N, 128, 512 * O)}
def setup_inputs_swap(rng):
    d = setup_inputs(rng); p = rng.permutation(N); dest = np.zeros((N, T), int)
    for k in range(N): dest[p[k]] = p[(k + 1) % N]
    d["to"] = places(rng, dest); return d
def setup_inputs_ones(rng):
    d = setup_inputs(rng); i = np.arange(N); n = np.ones((N, N), int); n[i, rng.permutation(N)] += T % N
    for t in range(T // N - 1): n[i, rng.permutation(N)] += N
    d["to"] = places(rng, np.stack([rng.permutation(np.repeat(i, n[r])) for r in range(N)])); return d
def setup_inputs_runs(rng):
    d = setup_inputs(rng); p = relabel(rng); s, u = rng.integers(1, N), rng.integers(0, N); g, h = rng.permutation(N), rng.permutation(N)
    n = T // N + ((g[:, None] + h) % N < T % N)
    j = (np.arange(N) + s * np.arange(N)[:, None] + u) % N
    d["to"] = places(rng, np.stack([np.repeat(p[j[r]], n[r, j[r]]) for r in range(N)])); return d
def setup_inputs_comb(rng):
    d = setup_inputs(rng); p = relabel(rng); s, u = rng.integers(1, N), rng.integers(0, N); k = rng.permutation(N); c = np.arange(T)
    d["to"] = places(rng, np.stack([p[(c + np.where(c < T - T % N, s * r + u, k[r])) % N] for r in range(N)])); return d
def setup_inputs_spread(rng):
    d = setup_inputs(rng); d["x"] = wide(rng, N, 128, 4 * T, cols=8); return d
def check_inputs(d):
    e = np.concatenate([entries(d["to"][r]) for r in range(N)])
    return [] if np.array_equal(np.sort(e), np.arange(N * T)) else ["to"]
def reference(x, to, w):
    z = np.concatenate([x[r] for r in range(N)], axis=1)
    e = np.concatenate([entries(to[r]) for r in range(N)])
    home = np.zeros(N * T, int); home[e] = np.arange(N * T)
    y = np.zeros((N, 128, O * T), np.float32)
    for d in range(N):
        v = mx_ref.quantize(cols(z, home[d * T:d * T + T]))
        for o in range(O): y[d][:, T * o:T * o + T] = mx_ref.matmul(mx_ref.quantize(np.ascontiguousarray(cut(w[d], o))), v)
    return {"y": y}

@@ -1,0 +1,352 @@
+from concourse.bass import DstId, RemoteDMATransfer
+from concourse.mybir import dt, AluOpType, ActivationFunctionType
+
+N, COLS, O = 4, 256, 2
+H = COLS // 2
+PK1 = COLS // N
+PK2 = COLS // N + N - 1
+ST = 80
+LC = ST // 16
+W1 = N * ST
+W2 = N * COLS
+NONE = -8192.0
+RND = 160.0
+MID = 128.0
+BUFFERS = {
+    "float8_e4m3fn_x4": "xq 256 wq 256 slot1q 192 land1q 256 slot2q 240 land2q 320 finq0 128 finq1 128",
+    "uint8": "xs 256 ws 256 slot1s 192 land1s 256 slot2s 240 land2s 320 fins0 128 fins1 128",
+    "bfloat16": "xb 1024 wb 1024 zb 64 restart 64 low0 64 val1 256 ec 32 ind 64 indt 64 cr 64 crt 64 cum 64 z 64 pp 64 pm 64 pm2 32 "
+                "bc 64 bt 64 win1 320 wt1 320 vt 16 prow 128 win2 1024 vo 64 vland 64 cn 4 cland 32 aa 20 aq 20 bu 4 bv 4",
+    "float32": "odd 1 odd5 1 odd8 1 bth 1 bcc 1 start 1 q0 1 q1 1 lowf 1 selm 1 sela 1 selb 1 tti 5 ttl 5 twi 80 ttw 80 cji 4 cj 4 "
+               "bv4 4 bd 4 bg 4 be 4 bs 4 r64 4 r64b 4 pos 16 t1 16 t2 16 eb 21 lo 20 hi 20 sf 20 xx 20 dd 20 ge 64 h1 84 h2 40 h3 20 "
+               "e80 4 q320 4 th 4 xa 4 cc 4 kk 64 f1 64 f2 32 f3 32 f3t 32 f4 16 yb0 256 yb1 256",
+    "int32": "part 1 par 1 low 1 mq 1 gm 1 la 1 lb 1 bit 1 ew 16 si 16 cb 30 pb 30 selk 4",
+    "uint16": "off1 16 l1u 16 eu 16 l2u 20 lou 6 flu 16 sel 2 selh 2 selz 4 bl 4",
+}
+SCRATCH = {"ps": ("psum", [128, 2048], "float32")}
+for _t, _l in BUFFERS.items():
+    _w = _l.split()
+    for _n, _c in zip(_w[0::2], _w[1::2]):
+        SCRATCH[_n] = ("sbuf", [128, int(_c)], _t)
+SEMAPHORES = "sv sa sg st ld_e ld_x ld_w vf vr vo vw cnt p1c p1s plc p2c p2s sent yo".split()
+
+
+def plan(src, cores, topo):
+    near = set(topo.cores_of(src))
+    far = [d for d in cores if d not in near]
+    close = [d for d in cores if d in near and d != src]
+    out, used = {}, set()
+    for group in (far, close):
+        if group:
+            eng = [e for e in topo.engines(src, group[0]) if e not in used]
+            per = len(eng) // len(group)
+            for i, d in enumerate(group):
+                out[d] = eng[per * i:per * (i + 1)]
+            used.update(eng)
+    return out
+
+
+def rank_program(g, core, T, topo):
+    me = T.rank_of(core)
+    if me is None:
+        return
+    A, F = AluOpType, ActivationFunctionType
+    S = T.sem
+    turn = [(me + 1 + i) % N for i in range(N)]
+    others = turn[:N - 1]
+    mine = plan(core, T.cores, topo)
+    arrive = sum(len(plan(T.cores[r], T.cores, topo)[core]) for r in others)
+    leave = sum(len(e) for e in mine.values())
+    v, s, te, sy = g.vector, g.scalar, g.tensor, g.sync
+    own_sem = {"v": "sv", "s": "sa", "g": "sg", "t": "st"}
+    queue = {"v": v, "s": s, "g": g, "t": te, "y": sy}
+    cnt = {k: 0 for k in SEMAPHORES}
+    made = {}
+    seen = {}
+
+    def hold(q, sem, k):
+        if seen.get((q, sem), 0) < k:
+            queue[q].wait_ge(S[sem], k)
+            seen[q, sem] = k
+
+    def need(q, *names):
+        for n in names:
+            for sem, k in made.get(n, {}).items():
+                hold(q, sem, k)
+
+    def ap(x):
+        return T[x][:] if not isinstance(x, tuple) else T[x[0]][:, slice(*x[1:])]
+
+    def name(x):
+        return x[0] if isinstance(x, tuple) else x
+
+    def named(*xs):
+        return [name(x) for x in xs if isinstance(x, (str, tuple))]
+
+    def val(x):
+        return ap(x) if isinstance(x, (str, tuple)) else x
+
+    def done(q, ins, out, sem=None, by=1):
+        sem = sem or own_sem[q]
+        ins.then_inc(S[sem], by)
+        cnt[sem] += by
+        for o in out:
+            made.setdefault(name(o), {})[sem] = cnt[sem]
+
+    def cp(out, i, q="v"):
+        need(q, name(i))
+        done(q, v.tensor_copy(ap(out), ap(i)) if q == "v" else s.activation(ap(out), ap(i), F.Copy), [out])
+
+    def tt(out, a, b, op, offs=None):
+        need("v", *named(a, b, offs))
+        a = ap(a) if offs is None else ap(a).indirect(ap(offs))
+        done("v", v.tensor_tensor(ap(out), a, ap(b), op), [out])
+
+    def ts(out, a, s1, op, s2=None, op2=None):
+        need("v", *named(a, s1, s2))
+        a, s1, s2 = ap(a), val(s1), val(s2)
+        done("v", v.tensor_scalar(ap(out), a, s1, s2, op, op2) if op2 else v.tensor_scalar(ap(out), a, s1, None, op), [out])
+
+    def tr(out, i):
+        need("v", i)
+        done("v", v.transpose(ap(out), ap(i)), [out])
+
+    def scan(out, a, b, initial, op0, op1):
+        need("v", *named(a, b, initial))
+        done("v", v.tensor_tensor_scan(ap(out), ap(a), ap(b), val(initial), op0, op1), [out])
+
+    def fill(x, c):
+        done("v", v.memset(ap(x), c), [x])
+
+    def iota(out, pat, base=0, cm=0, whole=False):
+        kw = {} if whole else {"allow_small_or_imprecise_dtypes": True}
+        done("g", g.iota(ap(out), pat, base, cm, **kw), [out])
+
+    def act(out, i, **kw):
+        need("s", *named(i, *kw.values()))
+        done("s", s.activation(ap(out), ap(i), F.Identity, **{k: val(x) for k, x in kw.items()}), [out])
+
+    def load(q, out, src, sem):
+        done(q, queue[q].dma_start(ap(out), src), [out], sem, 16)
+
+    def quant(k, a, b):
+        need("v", k + "b")
+        done("v", v.quantize_mx(ap((k + "q", a, b)), ap((k + "s", a, b)), ap((k + "b", 4 * a, 4 * b))), [k + "q", k + "s"])
+
+    def pick(q, out, win, offs):
+        need(q, win, name(offs))
+        if win[-1] == "q":
+            done(q, v.tensor_copy(ap(out).bitcast(dt.uint32), ap(win).bitcast(dt.uint32).indirect(ap(offs))), [out])
+        elif q == "v":
+            done(q, v.tensor_copy(ap(out), ap(win).indirect(ap(offs))), [out])
+        else:
+            done(q, s.activation(ap(out), ap(win).indirect(ap(offs)), F.Copy), [out])
+
+    def send(sem, buf, dst, cut, codes=False):
+        need("g", buf)
+        raw = (lambda t: t.bitcast(dt.uint8)) if codes else (lambda t: t)
+        tl = []
+        for d in others:
+            rid, pid = topo.addr(T.cores[d], core)
+            tl.append(RemoteDMATransfer(dst_ids=[DstId(rid=rid, pnc=pid)], dma_engine_mask=sum(1 << e for e in mine[T.cores[d]]),
+                                        remote_sem=S[sem], src=raw(ap((buf,) + cut(d))), dst=raw(ap(dst))))
+        g.remote_dma_fused(tl, local_sem=S.sent)
+        cnt["sent"] += leave
+        made.setdefault(name(dst), {})[sem] = arrive
+
+    for q, k0 in (("y", 0), ("s", 4)):
+        for k in range(k0, k0 + 4):
+            done(q, queue[q].dma_start(T.ew[16 * k:16 * k + 16, :], T.to[:, :]), ["ew"], "ld_e", 16)
+    load("y", "xb", T.x[:, :], "ld_x")
+    load("y", "wb", T.w[:, :], "ld_w")
+    fill("zb", 0.0)
+    fill(("win2", 0, COLS), NONE)
+    need("y", "win2")
+    for a in range(COLS, W2, COLS):
+        done("y", sy.dma_start(T.win2[:, a:a + COLS], T.win2[:, 0:COLS]), ["blank"], "vf", 16)
+
+    iota("part", [[1, 1]], 0, 1, True)
+    iota("selk", [[16, 4]], 15, 0, True)
+    iota("val1", [[1, 16], [16, 16]])
+    iota("cji", [[16, 4]])
+    iota("twi", [[-PK1, 4], [0, N], [16, LC]], -PK1)
+    iota("tti", [[16, LC]], -int(RND))
+    iota(("cb", 0, 10), [[0, 10]], 0, 0, True)
+    iota(("pb", 0, 10), [[0, 10]], 0, 0, True)
+    iota("r64", [[PK1, N]], int(RND + MID) - 1)
+    ts("par", "part", 4, A.logical_shift_right, 1, A.bitwise_and)
+    ts("low", "part", 15, A.bitwise_and)
+    ts("mq", "part", 2, A.logical_shift_right, 3, A.bitwise_and)
+    cp("odd", "par")
+    cp("lowf", "low")
+    tt("la", "low", "mq", A.add)
+    ts("gm", "low", 4 * (N - 1 - me) - 0.5, A.is_ge, -float(N * LC), A.mult)
+    ts("q0", "odd", 3.0, A.mult, RND, A.add)
+    ts("q1", "odd", RND + 1.0, A.add)
+    tt("lb", "la", "gm", A.add)
+    ts("bit", "lb", 1, A.bitwise_and)
+    flip = LC * (me + 1) % 2
+    act("sela", "odd", scale=16.0 - 64.0 * flip, bias=16.0 * LC * (me + 1) + 32.0 * flip)
+    act("selm", "odd", scale=-64.0 * (1 - 2 * flip), bias=32.0 * (1 - 2 * flip))
+    act("odd8", "odd", scale=8.0)
+    act("start", "odd", scale=-(COLS - 1.0))
+    act("restart", ("zb", 0, 64), bias=1.0)
+    act("low0", ("zb", 0, 64), bias=-NONE)
+    act("odd5", "odd", scale=1.0 / LC)
+    need("s", "restart", "low0")
+    act(("restart", 0, 64, 16), ("zb", 0, 4))
+    act(("low0", 16, 17), ("zb", 0, 1), bias=("start", 0, 1))
+    act("eb", ("zb", 0, 21))
+    act(("dd", 0, 5), ("zb", 0, 5))
+    act(("cn", 3, 4), ("zb", 0, 1), bias=float(COLS))
+    need("s", "eb")
+    act(("eb", 4, 20, 5), ("zb", 0, 4), bias=float(COLS))
+    act(("win1", 0, COLS), "val1", scale=0.0)
+    act(("win1", COLS, W1), ("zb", 0, W1 - COLS))
+    act("prow", ("val1", 0, H), scale=0.0)
+    ts("selb", "bit", ("selm", 0, 1), A.mult, ("sela", 0, 1), A.add)
+    cp("selz", "selk")
+    ts(("sel", 0, 1), "lb", 16.0, A.mult, ("selb", 0, 1), A.add)
+    ts(("selh", 0, 1), "low", ("odd8", 0, 1), A.add, 15.0, A.min)
+
+    for a in (0, 16):
+        ts(("ec", a, a + 16), "ew", 1.0 / COLS, A.mult, RND - 0.498, A.add)
+    for u in (0, 1):
+        ts(("ind", 32 * u, 32 * u + 32), "ec", ("q%d" % u, 0, 1), A.is_equal)
+    tr("indt", "ind")
+    scan("cr", "restart", "indt", 0.0, A.mult, A.add)
+    tr("crt", "cr")
+    scan(("cum", 0, 48), ("low0", 0, 48), ("crt", 0, 48), ("start", 0, 1), A.min, A.add)
+    scan(("cum", 48, 64), ("low0", 48, 64), ("crt", 48, 64), ("cum", 31, 32), A.min, A.add)
+    tr("z", "cum")
+    tt("pp", "z", "cr", A.subtract, "selz")
+    for i, c in enumerate((31, 47)):
+        act(("bc", 32 * i, 32 * i + 32), ("zb", 0, 32), bias=("cum", c, c + 1))
+    tt("pm", "pp", "indt", A.mult)
+    tr("bt", "bc")
+    tt("pm2", ("pm", 0, 32), ("pm", 32, 64), A.add)
+    tt("pos", ("pm2", 0, 16), ("pm2", 16, 32), A.subtract)
+    ts("si", "pos", 0.25, A.mult, -0.375, A.add)
+    ts("t1", "si", -(4.0 * ST - 1) / ST, A.mult, ("odd5", 0, 1), A.add)
+    tt("t2", "pos", "t1", A.add)
+    ts("off1", "t2", float(ST), A.mult)
+
+    act(("cn", 0, 3), ("bt", 15, 48, 16))
+    cp(("cland", 8 * me, 8 * me + 4), "cn", "s")
+    act("vt", "t2", scale=float(ST), bias=-MID)
+    for q, a, r in (("y", 0, 0), ("s", 24, 16)):
+        need(q, "vt", "prow")
+        for p in range(0, 128, 32):
+            done(q, queue[q].dma_start(T.prow[p + r:p + r + 1, :], T.vt[p + a:p + a + 8, :]), ["rows"], "vr", 16)
+    act("cj", "cji", bias="lowf")
+    act("ttl", "tti", bias="lowf")
+    act("ttw", "twi", bias="lowf")
+    act("bu", "cj", scale=0.2, bias=RND - 0.4)
+    act("bv", "cj", scale=0.05, bias=RND - 0.475)
+    act("bth", "odd", scale=16.0, bias=-MID - 0.5)
+    act("bcc", "odd", scale=-16.0)
+    act("bv4", "bv", scale=-4.0, bias=4 * RND)
+
+    need("v", "val1", "off1", "win1")
+    done("v", v.tensor_copy(T.win1[:, 0:W1].indirect(T.off1[:, 0:16]), T.val1[:, 0:COLS]), ["win1"])
+    quant("x", 0, H)
+    tr("wt1", "win1")
+    quant("x", H, COLS)
+    need("v", "wt1", "sel")
+    done("v", v.tensor_copy(T.l1u[:], T.wt1[:, 0:W1].indirect(T.sel[:, 0:1])), ["l1u"])
+    a1, b1 = PK1 * me, PK1 * (me + 1)
+    mix, own = ("l1u", 0, 12), ("l1u", 12, 16)
+    pick("v", "slot1q", "xq", mix)
+    pick("s", "slot1s", "xs", mix)
+    pick("s", ("land1s", a1, b1), "xs", own)
+
+    send("cnt", "cn", ("cland", 8 * me, 8 * me + 4), lambda d: (0, 4))
+    cut1 = lambda d: (PK1 * others.index(d), PK1 * (others.index(d) + 1))
+    send("p1c", "slot1q", ("land1q", a1, b1), cut1, True)
+    send("p1s", "slot1s", ("land1s", a1, b1), cut1)
+
+    need("v", "ew", "selh")
+    done("v", v.tensor_copy(T.eu[:], T.ew[:, 0:16].indirect(T.selh[:, 0:1])), ["eu"])
+    need("v", "rows", "prow", "eu", "win2", "blank")
+    done("v", v.tensor_copy(T.win2[:, 0:W2].indirect(T.eu[:, 0:8]), T.prow[:, 0:H]), ["win2"])
+    need("y", "win2")
+    for d in turn:
+        out = ("vo", 16 * d, 16 * d + 16) if d != me else ("vland", 16 * d, 16 * d + 16)
+        done("y", sy.dma_start(ap(out), T.win2[0:128:16, COLS * d:COLS * d + COLS]), [out], "vo" if d != me else "vw", 16)
+    send("plc", "vo", ("vland", 16 * me, 16 * me + 16), lambda d: (16 * d, 16 * d + 16))
+
+    for i, q, kw in ((0, 1, {}), (2, 2, {}), (1, 3, {"scale": -1.0, "bias": 1.0})):
+        act(("eb", q, 20, 5), ("cland", i, 32, 8), **kw)
+    act("lo", ("eb", 0, 20), scale=0.25)
+    act("hi", ("eb", 1, 21), scale=0.25, bias=0.375 - PK1)
+    act("aa", ("eb", 0, 20), scale=0.25, bias=RND + (N - 1 - me) / 4.0 - 0.375)
+    for x, d in enumerate(turn):
+        act(("h1", LC * x, LC * x + LC), "ttl", bias=("aa", d, d + 1))
+    act("aq", ("eb", 0, 20), scale=0.25, bias=RND - 0.375)
+    act("e80", ("eb", me, 20, 5), scale=float(ST), bias="bth")
+    act("q320", ("aq", me, 20, 5), scale=4.0 * ST, bias=-4.0 * ST * RND)
+    act("r64b", "r64", bias="bcc")
+
+    tt("bd", "bu", "bv4", A.add)
+    tt("be", "bu", "bv", A.add)
+    tt(("cb", 10, 30), "hi", "lo", A.subtract)
+    ts("bg", "bd", RND + 2.5 - me, A.is_ge, -float(N), A.mult)
+    tt(("pb", 10, 30), ("cb", 5, 25), ("cb", 0, 20), A.add)
+    tt("bs", "be", "bg", A.add)
+    tt("sf", ("pb", 10, 30), ("pb", 0, 20), A.add)
+    ts("bl", "bs", me + 6.0 - 2 * RND, A.add, 19.0, A.min)
+    tt("xx", "aa", "sf", A.subtract)
+    tt("ge", "sf", ("ttw", 0, 64), A.is_le, "bl")
+    tt(("dd", 5, 20), ("xx", 5, 20), ("xx", 0, 15), A.subtract)
+    pick("v", ("land1q", a1, b1), "xq", own)
+    tt(("h1", 20, 84), "dd", "ge", A.mult, "bl")
+    tt("h2", ("h1", 0, 40), ("h1", 40, 80), A.add)
+    tt("h3", ("h2", 0, 20), ("h2", 20, 40), A.add)
+    ts("l2u", "h3", float(COLS - 1), A.min)
+
+    own2 = (ST * me, ST * me + ST)
+    pk2 = (ST * me, ST * me + PK2)
+    pick("v", "slot2q", "land1q", ("l2u", 0, 3 * LC))
+    ts(("lou", 0, LC), ("h3", 3 * LC, 4 * LC), float(COLS - 1), A.min)
+    tt("xa", ("sf", me, 20, 5), ("aq", me, 20, 5), A.subtract)
+    pick("v", ("land2q",) + own2, "land1q", ("lou", 0, LC))
+    pick("s", "slot2s", "land1s", ("l2u", 0, 3 * LC))
+    pick("s", ("land2s",) + own2, "land1s", ("lou", 0, LC))
+    cut2 = lambda d: (ST * others.index(d), ST * others.index(d) + PK2)
+    send("p2c", "slot2q", ("land2q",) + pk2, cut2, True)
+    send("p2s", "slot2s", ("land2s",) + pk2, cut2)
+
+    tt("th", "e80", "q320", A.subtract)
+    tt("cc", "xa", "r64b", A.add)
+    quant("w", 0, COLS)
+    for r in range(N):
+        ts(("kk", 16 * r, 16 * r + 16), ("vland", 16 * r, 16 * r + 16), ("th", r, r + 1), A.is_ge, ("cc", r, r + 1), A.add)
+    tt("f1", "vland", "kk", A.add)
+    tt("f2", ("f1", 0, 32), ("f1", 32, 64), A.max)
+    for a in (0, 16):
+        tt(("f3", a, a + 16), ("f2", 0, 16), ("f2", 16, 32), A.max)
+    tr("f3t", "f3")
+    tt("f4", ("f3t", 0, 16), ("f3t", 16, 32), A.max)
+    cp("flu", "f4")
+
+    for h in (0, 1):
+        pick("v", "finq%d" % h, "land2q", ("flu", 8 * h, 8 * h + 8))
+    for h, q in enumerate("sv"):
+        pick(q, "fins%d" % h, "land2s", ("flu", 8 * h, 8 * h + 8))
+    for o in range(O):
+        for h in (0, 1):
+            need("t", "finq%d" % h, "fins%d" % h, "wq", "ws")
+            p, wc = 512 * (2 * o + h), (128 * o, 128 * o + 128)
+            done("t", te.matmul_mx(T.ps[:, p:p + H], ap(("wq",) + wc), ap(("ws",) + wc), ap("finq%d" % h), ap("fins%d" % h),
+                                   True, True), ["ps%d" % p])
+    for o in range(O):
+        for h, q in enumerate("sv"):
+            p, y = 512 * (2 * o + h), ("yb%d" % o, H * h, H * h + H)
+            need(q, "ps%d" % p)
+            done(q, v.tensor_copy(ap(y), T.ps[:, p:p + H]) if q == "v" else s.activation(ap(y), T.ps[:, p:p + H], F.Copy), [y])
+    for o, q in enumerate("ys"):
+        need(q, "yb%d" % o)
+        done(q, queue[q].dma_start(T.y[:, COLS * o:COLS * o + COLS], T["yb%d" % o][:]), ["out"], "yo", 16)
+    hold("y", "yo", cnt["yo"])
+    hold("g", "sent", cnt["sent"])
+    hold("g", "sg", cnt["sg"])

@@ -7,28 +7,30 @@ PK1 = COLS // N
 PK2 = COLS // N + N - 1
 ST = 80
 LC = ST // 16
-W1 = N * ST
-W2 = N * COLS
+W1 = COLS + 32
+A2 = (N - 1) * COLS
 NONE = -8192.0
 RND = 160.0
 MID = 128.0
+ORDER = (0, 2, 3, 1)
+UP8 = 3 - 8 * PK1
 BUFFERS = {
     "float8_e4m3fn_x4": "xq 256 wq 256 slot1q 192 land1q 256 slot2q 240 land2q 320 finq0 128 finq1 128",
     "uint8": "xs 256 ws 256 slot1s 192 land1s 256 slot2s 240 land2s 320 fins0 128 fins1 128",
-    "bfloat16": "xb 1024 wb 1024 zb 64 restart 64 low0 64 val1 256 ec 32 ind 64 indt 64 cr 64 crt 64 cum 64 z 64 pp 64 pm 64 pm2 32 "
-                "bc 64 bt 64 win1 320 wt1 320 vt 16 prow 128 win2 1024 vo 64 vland 64 cn 4 cland 32 aa 20 aq 20 bu 4 bv 4",
-    "float32": "odd 1 odd5 1 odd8 1 bth 1 bcc 1 start 1 q0 1 q1 1 lowf 1 selm 1 sela 1 selb 1 tti 5 ttl 5 twi 80 ttw 80 cji 4 cj 4 "
-               "bv4 4 bd 4 bg 4 be 4 bs 4 r64 4 r64b 4 pos 16 t1 16 t2 16 eb 21 lo 20 hi 20 sf 20 xx 20 dd 20 ge 64 h1 84 h2 40 h3 20 "
-               "e80 4 q320 4 th 4 xa 4 cc 4 kk 64 f1 64 f2 32 f3 32 f3t 32 f4 16 yb0 256 yb1 256",
-    "int32": "part 1 par 1 low 1 mq 1 gm 1 la 1 lb 1 bit 1 ew 16 si 16 cb 30 pb 30 selk 4",
-    "uint16": "off1 16 l1u 16 eu 16 l2u 20 lou 6 flu 16 sel 2 selh 2 selz 4 bl 4",
+    "bfloat16": "xb 1024 wb 1024 restart 64 low0 128 cls 64 ec 16 ind 64 cr 64 crt 128 cum 128 z 128 pp 64 "
+                "win1 288 wt1 288 tab 256 prow 256 win2 1808 wt2 288 vland 64 cn 4 cland 24 aa 16 aq 4",
+    "float32": "idt 288 partf 1 odd 2 lowf 1 y16 1 sh1 1 sh2 1 shift 1 offb 1 odd16 1 cjk 8 e8 20 ebs 20 twi 80 ttw 80 indc 64 "
+               "pm 64 pm2 32 eb 17 sf 20 da 12 dd 20 ge 64 h1 84 h2 40 h3 20 e64 4 q256 4 th 4 xa 4 cc 4 kk 64 f0 64 "
+               "f1 64 f2 32 f3 16 yb0 256 yb1 256",
+    "int32": "part 4 par 2 low 4 yy 2 yo 2 ew 16 pos 16 num 16 cb 24 pb 24 selk 4",
+    "uint16": "off1 16 off0 16 l1u 32 eu 16 l2u 16 lou 6 flu 16 sel 2 selz 4 rep 4 bl 8",
 }
 SCRATCH = {"ps": ("psum", [128, 2048], "float32")}
 for _t, _l in BUFFERS.items():
     _w = _l.split()
     for _n, _c in zip(_w[0::2], _w[1::2]):
         SCRATCH[_n] = ("sbuf", [128, int(_c)], _t)
-SEMAPHORES = "sv sa sg st ld_e ld_x ld_w vf vr vo vw cnt p1c p1s plc p2c p2s sent yo".split()
+SEMAPHORES = "sv sa sg st ld_e ld_x ld_w cnt p1c p1s plc p2c p2s sent out".split()
 
 
 def plan(src, cores, topo):
@@ -43,7 +45,8 @@ def plan(src, cores, topo):
             for i, d in enumerate(group):
                 out[d] = eng[per * i:per * (i + 1)]
             used.update(eng)
-    return out
+    least = min(len(e) for e in out.values())
+    return {d: e[::len(e) // least] for d, e in out.items()}
 
 
 def rank_program(g, core, T, topo):
@@ -54,6 +57,8 @@ def rank_program(g, core, T, topo):
     S = T.sem
     turn = [(me + 1 + i) % N for i in range(N)]
     others = turn[:N - 1]
+    at = ORDER.index(me)
+    others2 = [ORDER[(at + 1 + i) % N] for i in range(N - 1)]
     mine = plan(core, T.cores, topo)
     arrive = sum(len(plan(T.cores[r], T.cores, topo)[core]) for r in others)
     leave = sum(len(e) for e in mine.values())
@@ -86,6 +91,9 @@ def rank_program(g, core, T, topo):
     def val(x):
         return ap(x) if isinstance(x, (str, tuple)) else x
 
+    def via(x, offs):
+        return ap(x) if offs is None else ap(x).indirect(ap(offs))
+
     def done(q, ins, out, sem=None, by=1):
         sem = sem or own_sem[q]
         ins.then_inc(S[sem], by)
@@ -93,14 +101,17 @@ def rank_program(g, core, T, topo):
         for o in out:
             made.setdefault(name(o), {})[sem] = cnt[sem]
 
-    def cp(out, i, q="v"):
-        need(q, name(i))
-        done(q, v.tensor_copy(ap(out), ap(i)) if q == "v" else s.activation(ap(out), ap(i), F.Copy), [out])
+    def cp(out, i, offs=None):
+        need("v", *named(i, offs))
+        done("v", v.tensor_copy(ap(out), via(i, offs)), [out])
+
+    def scatter(win, offs, i):
+        need("v", *named(win, offs, i))
+        done("v", v.tensor_copy(via(win, offs), ap(i)), [win])
 
     def tt(out, a, b, op, offs=None):
         need("v", *named(a, b, offs))
-        a = ap(a) if offs is None else ap(a).indirect(ap(offs))
-        done("v", v.tensor_tensor(ap(out), a, ap(b), op), [out])
+        done("v", v.tensor_tensor(ap(out), via(a, offs), ap(b), op), [out])
 
     def ts(out, a, s1, op, s2=None, op2=None):
         need("v", *named(a, s1, s2))
@@ -108,7 +119,7 @@ def rank_program(g, core, T, topo):
         done("v", v.tensor_scalar(ap(out), a, s1, s2, op, op2) if op2 else v.tensor_scalar(ap(out), a, s1, None, op), [out])
 
     def tr(out, i):
-        need("v", i)
+        need("v", name(i))
         done("v", v.transpose(ap(out), ap(i)), [out])
 
     def scan(out, a, b, initial, op0, op1):
@@ -122,9 +133,9 @@ def rank_program(g, core, T, topo):
         kw = {} if whole else {"allow_small_or_imprecise_dtypes": True}
         done("g", g.iota(ap(out), pat, base, cm, **kw), [out])
 
-    def act(out, i, **kw):
-        need("s", *named(i, *kw.values()))
-        done("s", s.activation(ap(out), ap(i), F.Identity, **{k: val(x) for k, x in kw.items()}), [out])
+    def act(out, i, offs=None, **kw):
+        need("s", *named(i, offs, *kw.values()))
+        done("s", s.activation(ap(out), via(i, offs), F.Identity, **{k: val(x) for k, x in kw.items()}), [out])
 
     def load(q, out, src, sem):
         done(q, queue[q].dma_start(ap(out), src), [out], sem, 16)
@@ -138,9 +149,9 @@ def rank_program(g, core, T, topo):
         if win[-1] == "q":
             done(q, v.tensor_copy(ap(out).bitcast(dt.uint32), ap(win).bitcast(dt.uint32).indirect(ap(offs))), [out])
         elif q == "v":
-            done(q, v.tensor_copy(ap(out), ap(win).indirect(ap(offs))), [out])
+            done(q, v.tensor_copy(ap(out), via(win, offs)), [out])
         else:
-            done(q, s.activation(ap(out), ap(win).indirect(ap(offs)), F.Copy), [out])
+            done(q, s.activation(ap(out), via(win, offs), F.Copy), [out])
 
     def send(sem, buf, dst, cut, codes=False):
         need("g", buf)
@@ -152,182 +163,149 @@ def rank_program(g, core, T, topo):
                                         remote_sem=S[sem], src=raw(ap((buf,) + cut(d))), dst=raw(ap(dst))))
         g.remote_dma_fused(tl, local_sem=S.sent)
         cnt["sent"] += leave
-        made.setdefault(name(dst), {})[sem] = arrive
+        cnt[sem] += arrive
+        made.setdefault(name(dst), {})[sem] = cnt[sem]
 
     for q, k0 in (("y", 0), ("s", 4)):
         for k in range(k0, k0 + 4):
             done(q, queue[q].dma_start(T.ew[16 * k:16 * k + 16, :], T.to[:, :]), ["ew"], "ld_e", 16)
     load("y", "xb", T.x[:, :], "ld_x")
     load("y", "wb", T.w[:, :], "ld_w")
-    fill("zb", 0.0)
-    fill(("win2", 0, COLS), NONE)
-    need("y", "win2")
-    for a in range(COLS, W2, COLS):
-        done("y", sy.dma_start(T.win2[:, a:a + COLS], T.win2[:, 0:COLS]), ["blank"], "vf", 16)
 
-    iota("part", [[1, 1]], 0, 1, True)
-    iota("selk", [[16, 4]], 15, 0, True)
-    iota("val1", [[1, 16], [16, 16]])
-    iota("cji", [[16, 4]])
+    iota("part", [[0, 4]], 0, 1, True)
+    iota("cls", [[1, N], [0, 16]], int(RND))
+    iota("selk", [[64, 2], [16, 2]], 15, 0, True)
+    iota("cjk", [[N * LC, 2], [16, 4]], -2)
+    iota("partf", [[0, 1]], 0, 1)
+    iota("idt", [[1, W1]])
+    iota("tab", [[ST, N], [1, PK1]], -int(MID))
+    iota("e8", [[8 * PK1 + N * UP8, 5], [UP8, N]])
     iota("twi", [[-PK1, 4], [0, N], [16, LC]], -PK1)
-    iota("tti", [[16, LC]], -int(RND))
-    iota(("cb", 0, 10), [[0, 10]], 0, 0, True)
-    iota(("pb", 0, 10), [[0, 10]], 0, 0, True)
-    iota("r64", [[PK1, N]], int(RND + MID) - 1)
-    ts("par", "part", 4, A.logical_shift_right, 1, A.bitwise_and)
+    fill("low0", -NONE)
+    fill("restart", -NONE)
+    fill("crt", 0.0)
+    ts("par", ("part", 0, 2), 4, A.logical_shift_right, 1, A.bitwise_and)
     ts("low", "part", 15, A.bitwise_and)
-    ts("mq", "part", 2, A.logical_shift_right, 3, A.bitwise_and)
     cp("odd", "par")
-    cp("lowf", "low")
-    tt("la", "low", "mq", A.add)
-    ts("gm", "low", 4 * (N - 1 - me) - 0.5, A.is_ge, -float(N * LC), A.mult)
-    ts("q0", "odd", 3.0, A.mult, RND, A.add)
-    ts("q1", "odd", RND + 1.0, A.add)
-    tt("lb", "la", "gm", A.add)
-    ts("bit", "lb", 1, A.bitwise_and)
-    flip = LC * (me + 1) % 2
-    act("sela", "odd", scale=16.0 - 64.0 * flip, bias=16.0 * LC * (me + 1) + 32.0 * flip)
-    act("selm", "odd", scale=-64.0 * (1 - 2 * flip), bias=32.0 * (1 - 2 * flip))
-    act("odd8", "odd", scale=8.0)
-    act("start", "odd", scale=-(COLS - 1.0))
-    act("restart", ("zb", 0, 64), bias=1.0)
-    act("low0", ("zb", 0, 64), bias=-NONE)
-    act("odd5", "odd", scale=1.0 / LC)
-    need("s", "restart", "low0")
-    act(("restart", 0, 64, 16), ("zb", 0, 4))
-    act(("low0", 16, 17), ("zb", 0, 1), bias=("start", 0, 1))
-    act("eb", ("zb", 0, 21))
-    act(("dd", 0, 5), ("zb", 0, 5))
-    act(("cn", 3, 4), ("zb", 0, 1), bias=float(COLS))
-    need("s", "eb")
-    act(("eb", 4, 20, 5), ("zb", 0, 4), bias=float(COLS))
-    act(("win1", 0, COLS), "val1", scale=0.0)
-    act(("win1", COLS, W1), ("zb", 0, W1 - COLS))
-    act("prow", ("val1", 0, H), scale=0.0)
-    ts("selb", "bit", ("selm", 0, 1), A.mult, ("sela", 0, 1), A.add)
+    fill(("restart", 0, 64, 16), 0.0)
+    cp("lowf", ("low", 0, 1))
+    cp("rep", "low")
+    ts(("low0", 16, 17), ("par", 0, 1), -(COLS - 1.0), A.mult)
+    fill(("cn", 0, 1), 0.0)
     cp("selz", "selk")
-    ts(("sel", 0, 1), "lb", 16.0, A.mult, ("selb", 0, 1), A.add)
-    ts(("selh", 0, 1), "low", ("odd8", 0, 1), A.add, 15.0, A.min)
+    odd = ("odd", 0, 1)
+    act("odd16", odd, scale=16.0)
+    act("sh1", "lowf", scale=8.0, bias=float(A2))
+    act("sh2", odd, scale=144.0, bias="sh1")
+    act("shift", "partf", scale=-8.0, bias="sh2")
+    tt("yy", ("low", 0, 2), "par", A.subtract)
+    fill(("cb", 0, 8), 0)
+    ts("yo", "yy", 1, A.bitwise_and)
+    ts("y16", ("yy", 0, 1), 16.0, A.mult)
+    fill(("pb", 0, 8), 0)
+    ts("sel", "yo", 32.0, A.mult, "y16", A.add)
+    ts("bl", "cjk", "lowf", A.add, 0.2, A.mult)
 
-    for a in (0, 16):
-        ts(("ec", a, a + 16), "ew", 1.0 / COLS, A.mult, RND - 0.498, A.add)
+    ts("ec", "ew", 1.0 / COLS, A.mult, RND - 0.498, A.add)
+    tt("ind", "ec", "cls", A.is_equal, "rep")
+    scan("cr", "restart", "ind", 0.0, A.min, A.add)
+    act("indc", "ind", scale=COLS + 1.0)
     for u in (0, 1):
-        ts(("ind", 32 * u, 32 * u + 32), "ec", ("q%d" % u, 0, 1), A.is_equal)
-    tr("indt", "ind")
-    scan("cr", "restart", "indt", 0.0, A.mult, A.add)
-    tr("crt", "cr")
-    scan(("cum", 0, 48), ("low0", 0, 48), ("crt", 0, 48), ("start", 0, 1), A.min, A.add)
-    scan(("cum", 48, 64), ("low0", 48, 64), ("crt", 48, 64), ("cum", 31, 32), A.min, A.add)
+        tr(("crt", 64 * u, 64 * u + 32), ("cr", 32 * u, 32 * u + 32))
+    scan(("cum", 0, 80), ("low0", 0, 80), ("crt", 0, 80), ("low0", 16, 17), A.min, A.add)
+    scan(("cum", 80, 128), ("low0", 80, 128), ("crt", 80, 128), ("cum", 63, 64), A.min, A.add)
     tr("z", "cum")
     tt("pp", "z", "cr", A.subtract, "selz")
-    for i, c in enumerate((31, 47)):
-        act(("bc", 32 * i, 32 * i + 32), ("zb", 0, 32), bias=("cum", c, c + 1))
-    tt("pm", "pp", "indt", A.mult)
-    tr("bt", "bc")
+    ts(("cn", 1, 3), ("z", 47, 112, 64), 0.25, A.mult)
+    ts(("cn", 3, 4), ("z", 63, 64), -0.25, A.mult, 0.25, A.add)
+    mine4 = ("cland", 4 * me, 4 * me + 4)
+    need("y", "cn")
+    load("y", mine4, T.cn[:], "cnt")
+    send("cnt", "cn", mine4, lambda d: (0, 4))
+    tt("pm", "pp", "indc", A.mult)
+    ts("eu", "ew", "shift", A.add)
     tt("pm2", ("pm", 0, 32), ("pm", 32, 64), A.add)
     tt("pos", ("pm2", 0, 16), ("pm2", 16, 32), A.subtract)
-    ts("si", "pos", 0.25, A.mult, -0.375, A.add)
-    ts("t1", "si", -(4.0 * ST - 1) / ST, A.mult, ("odd5", 0, 1), A.add)
-    tt("t2", "pos", "t1", A.add)
-    ts("off1", "t2", float(ST), A.mult)
-
-    act(("cn", 0, 3), ("bt", 15, 48, 16))
-    cp(("cland", 8 * me, 8 * me + 4), "cn", "s")
-    act("vt", "t2", scale=float(ST), bias=-MID)
-    for q, a, r in (("y", 0, 0), ("s", 24, 16)):
-        need(q, "vt", "prow")
-        for p in range(0, 128, 32):
-            done(q, queue[q].dma_start(T.prow[p + r:p + r + 1, :], T.vt[p + a:p + a + 8, :]), ["rows"], "vr", 16)
-    act("cj", "cji", bias="lowf")
-    act("ttl", "tti", bias="lowf")
+    ts("num", "pos", 2, A.logical_shift_right, COLS - 1, A.bitwise_and)
+    ts("off1", "num", "odd16", A.add)
+    cp("off0", "num")
+    act("win1", "idt", scale=0.0)
+    act("ebs", "e8", scale=0.125)
     act("ttw", "twi", bias="lowf")
-    act("bu", "cj", scale=0.2, bias=RND - 0.4)
-    act("bv", "cj", scale=0.05, bias=RND - 0.475)
-    act("bth", "odd", scale=16.0, bias=-MID - 0.5)
-    act("bcc", "odd", scale=-16.0)
-    act("bv4", "bv", scale=-4.0, bias=4 * RND)
+    act("prow", "tab", "off0")
+    act(("win2", A2, A2 + W1), "idt", scale=0.0, bias=NONE)
+    for x in (("dd", 0, 4), ("dd", 16, 20), ("sf", 16, 20), ("cland", 16, 20)):
+        act(x, ("idt", 0, 4), scale=0.0)
 
-    need("v", "val1", "off1", "win1")
-    done("v", v.tensor_copy(T.win1[:, 0:W1].indirect(T.off1[:, 0:16]), T.val1[:, 0:COLS]), ["win1"])
+    scatter("win1", "off1", ("idt", 0, COLS))
     quant("x", 0, H)
     tr("wt1", "win1")
     quant("x", H, COLS)
-    need("v", "wt1", "sel")
-    done("v", v.tensor_copy(T.l1u[:], T.wt1[:, 0:W1].indirect(T.sel[:, 0:1])), ["l1u"])
+    cp("l1u", "wt1", "sel")
     a1, b1 = PK1 * me, PK1 * (me + 1)
-    mix, own = ("l1u", 0, 12), ("l1u", 12, 16)
+    mix, own = ("l1u", 4 * me + 4, 4 * me + 16), ("l1u", 4 * me, 4 * me + 4)
     pick("v", "slot1q", "xq", mix)
     pick("s", "slot1s", "xs", mix)
     pick("s", ("land1s", a1, b1), "xs", own)
-
-    send("cnt", "cn", ("cland", 8 * me, 8 * me + 4), lambda d: (0, 4))
     cut1 = lambda d: (PK1 * others.index(d), PK1 * (others.index(d) + 1))
     send("p1c", "slot1q", ("land1q", a1, b1), cut1, True)
     send("p1s", "slot1s", ("land1s", a1, b1), cut1)
 
-    need("v", "ew", "selh")
-    done("v", v.tensor_copy(T.eu[:], T.ew[:, 0:16].indirect(T.selh[:, 0:1])), ["eu"])
-    need("v", "rows", "prow", "eu", "win2", "blank")
-    done("v", v.tensor_copy(T.win2[:, 0:W2].indirect(T.eu[:, 0:8]), T.prow[:, 0:H]), ["win2"])
-    need("y", "win2")
-    for d in turn:
-        out = ("vo", 16 * d, 16 * d + 16) if d != me else ("vland", 16 * d, 16 * d + 16)
-        done("y", sy.dma_start(ap(out), T.win2[0:128:16, COLS * d:COLS * d + COLS]), [out], "vo" if d != me else "vw", 16)
-    send("plc", "vo", ("vland", 16 * me, 16 * me + 16), lambda d: (16 * d, 16 * d + 16))
+    scatter("win2", "eu", "prow")
 
-    for i, q, kw in ((0, 1, {}), (2, 2, {}), (1, 3, {"scale": -1.0, "bias": 1.0})):
-        act(("eb", q, 20, 5), ("cland", i, 32, 8), **kw)
-    act("lo", ("eb", 0, 20), scale=0.25)
-    act("hi", ("eb", 1, 21), scale=0.25, bias=0.375 - PK1)
-    act("aa", ("eb", 0, 20), scale=0.25, bias=RND + (N - 1 - me) / 4.0 - 0.375)
-    for x, d in enumerate(turn):
-        act(("h1", LC * x, LC * x + LC), "ttl", bias=("aa", d, d + 1))
-    act("aq", ("eb", 0, 20), scale=0.25, bias=RND - 0.375)
-    act("e80", ("eb", me, 20, 5), scale=float(ST), bias="bth")
-    act("q320", ("aq", me, 20, 5), scale=4.0 * ST, bias=-4.0 * ST * RND)
-    act("r64b", "r64", bias="bcc")
-
-    tt("bd", "bu", "bv4", A.add)
-    tt("be", "bu", "bv", A.add)
-    tt(("cb", 10, 30), "hi", "lo", A.subtract)
-    ts("bg", "bd", RND + 2.5 - me, A.is_ge, -float(N), A.mult)
-    tt(("pb", 10, 30), ("cb", 5, 25), ("cb", 0, 20), A.add)
-    tt("bs", "be", "bg", A.add)
-    tt("sf", ("pb", 10, 30), ("pb", 0, 20), A.add)
-    ts("bl", "bs", me + 6.0 - 2 * RND, A.add, 19.0, A.min)
-    tt("xx", "aa", "sf", A.subtract)
-    tt("ge", "sf", ("ttw", 0, 64), A.is_le, "bl")
-    tt(("dd", 5, 20), ("xx", 5, 20), ("xx", 0, 15), A.subtract)
+    act("aa", ("cland", 0, 16), bias=RND + (N - 1 - me) / 4.0 - 0.375)
+    tt("eb", ("cland", 0, 17), ("ebs", 0, 17), A.add)
+    tr("wt2", ("win2", A2, A2 + W1))
+    tt(("cb", 8, 24), ("eb", 1, 17), ("eb", 0, 16), A.subtract)
+    mine16 = (16 * me, 16 * me + 16)
+    cp(("vland",) + mine16, "wt2", ("sel", 0, 1))
+    send("plc", "vland", ("vland",) + mine16, lambda d: mine16)
+    tt("da", ("aa", 4, 16), ("aa", 0, 12), A.subtract)
+    tt(("pb", 8, 24), ("cb", 4, 20), ("cb", 0, 16), A.add)
+    tt(("dd", 4, 16), "da", ("cb", 8, 20), A.subtract)
+    tt(("sf", 0, 16), ("pb", 8, 24), ("pb", 0, 16), A.add)
+    tt(("h1", 0, 32), "aa", ("ttw", 0, 32), A.add, ("bl", 0, 2))
+    tt("ge", "sf", ("ttw", 0, 64), A.is_le, ("bl", 4, 8))
     pick("v", ("land1q", a1, b1), "xq", own)
-    tt(("h1", 20, 84), "dd", "ge", A.mult, "bl")
+    tt(("h1", 20, 84), "dd", "ge", A.mult, ("bl", 4, 8))
     tt("h2", ("h1", 0, 40), ("h1", 40, 80), A.add)
     tt("h3", ("h2", 0, 20), ("h2", 20, 40), A.add)
-    ts("l2u", "h3", float(COLS - 1), A.min)
+
+    def cut(out, a, b):
+        ts(out, ("h3", a, b), PK1 - RND, A.add, float(COLS - 1), A.min)
+    after = LC * (N - 1 - at)
+    if after:
+        cut(("l2u", 0, after), LC * (at + 1), LC * N)
+    if at:
+        cut(("l2u", after, after + LC * at), 0, LC * at)
+    base = ("cland", at, 16, 4)
+    act("aq", base, bias=RND - 0.375)
+    act("e64", base, scale=4.0 * ST, bias=-MID - 0.5)
+    act("q256", "aq", scale=4.0 * ST, bias=-4.0 * ST * RND)
 
     own2 = (ST * me, ST * me + ST)
     pk2 = (ST * me, ST * me + PK2)
     pick("v", "slot2q", "land1q", ("l2u", 0, 3 * LC))
-    ts(("lou", 0, LC), ("h3", 3 * LC, 4 * LC), float(COLS - 1), A.min)
-    tt("xa", ("sf", me, 20, 5), ("aq", me, 20, 5), A.subtract)
+    cut(("lou", 0, LC), LC * at, LC * at + LC)
+    tt("xa", ("sf", at, 16, 4), "aq", A.subtract)
     pick("v", ("land2q",) + own2, "land1q", ("lou", 0, LC))
     pick("s", "slot2s", "land1s", ("l2u", 0, 3 * LC))
     pick("s", ("land2s",) + own2, "land1s", ("lou", 0, LC))
-    cut2 = lambda d: (ST * others.index(d), ST * others.index(d) + PK2)
+    cut2 = lambda d: (ST * others2.index(d), ST * others2.index(d) + PK2)
     send("p2c", "slot2q", ("land2q",) + pk2, cut2, True)
     send("p2s", "slot2s", ("land2s",) + pk2, cut2)
 
-    tt("th", "e80", "q320", A.subtract)
-    tt("cc", "xa", "r64b", A.add)
+    tt("th", "e64", "q256", A.subtract)
+    tt("cc", "xa", ("idt", 0, COLS, PK1), A.add)
     quant("w", 0, COLS)
     for r in range(N):
         ts(("kk", 16 * r, 16 * r + 16), ("vland", 16 * r, 16 * r + 16), ("th", r, r + 1), A.is_ge, ("cc", r, r + 1), A.add)
     tt("f1", "vland", "kk", A.add)
     tt("f2", ("f1", 0, 32), ("f1", 32, 64), A.max)
-    for a in (0, 16):
-        tt(("f3", a, a + 16), ("f2", 0, 16), ("f2", 16, 32), A.max)
-    tr("f3t", "f3")
-    tt("f4", ("f3t", 0, 16), ("f3t", 16, 32), A.max)
-    cp("flu", "f4")
+    tt("f3", ("f2", 0, 16), ("f2", 16, 32), A.max)
+    need("v", "f3")
+    for p in range(0, 128, 32):
+        done("v", v.tensor_scalar(T.flu[p:p + 32, :], T.f3[32 * me:32 * me + 32, :], RND + MID - 1, None, A.add), ["flu"])
 
     for h in (0, 1):
         pick("v", "finq%d" % h, "land2q", ("flu", 8 * h, 8 * h + 8))
@@ -346,7 +324,7 @@ def rank_program(g, core, T, topo):
             done(q, v.tensor_copy(ap(y), T.ps[:, p:p + H]) if q == "v" else s.activation(ap(y), T.ps[:, p:p + H], F.Copy), [y])
     for o, q in enumerate("ys"):
         need(q, "yb%d" % o)
-        done(q, queue[q].dma_start(T.y[:, COLS * o:COLS * o + COLS], T["yb%d" % o][:]), ["out"], "yo", 16)
-    hold("y", "yo", cnt["yo"])
+        done(q, queue[q].dma_start(T.y[:, COLS * o:COLS * o + COLS], T["yb%d" % o][:]), ["stored"], "out", 16)
+    hold("y", "out", cnt["out"])
     hold("g", "sent", cnt["sent"])
     hold("g", "sg", cnt["sg"])

@@ -12,19 +12,24 @@ A2 = (N - 1) * COLS
 NONE = -8192.0
 RND = 160.0
 MID = 128.0
-ORDER = (0, 2, 3, 1)
-UP8 = 3 - 8 * PK1
+RUP = 128
 BUFFERS = {
     "float8_e4m3fn_x4": "xq 256 wq 256 slot1q 192 land1q 256 slot2q 240 land2q 320 finq0 128 finq1 128",
     "uint8": "xs 256 ws 256 slot1s 192 land1s 256 slot2s 240 land2s 320 fins0 128 fins1 128",
-    "bfloat16": "xb 1024 wb 1024 restart 64 low0 128 cls 64 ec 16 ind 64 cr 64 crt 128 cum 128 z 128 pp 64 "
-                "win1 288 wt1 288 tab 256 prow 256 win2 1808 wt2 288 vland 64 cn 4 cland 24 aa 16 aq 4",
-    "float32": "idt 288 partf 1 odd 2 lowf 1 y16 1 sh1 1 sh2 1 shift 1 offb 1 odd16 1 cjk 8 e8 20 ebs 20 twi 80 ttw 80 indc 64 "
-               "pm 64 pm2 32 eb 17 sf 20 da 12 dd 20 ge 64 h1 84 h2 40 h3 20 e64 4 q256 4 th 4 xa 4 cc 4 kk 64 f0 64 "
+    "bfloat16": "xb 1024 wb 1024 restart 48 low0 128 less 80 ind 80 wj 64 cr 64 crt 128 cum 128 z 128 "
+                "win1 288 wt1 288 tab 256 prow 128 win2 1808 wt2 544 mx 17 vland 64 cn 4 cland 24 aa 32 aq 4 cb 20 msk 20",
+    "float32": "idt 288 partf 1 odd 2 lowf 1 y16 1 y05 1 odd8 1 odd16 1 sh1 1 sh2 1 shift 1 c16 5 qi 35 ebs 35 twi 80 ttw 80 "
+               "d0i 80 d0 80 lowa 1 lowb 1 lqf 1 e4 2 k19 2 gf 2 aa2 20 thr 48 k16 16 c15 1 wt 96 wn 64 mm 64 zi 128 t1 64 t2 32 "
+               "eb 32 sf 20 da 20 dd 20 ge 80 h1 80 h3 80 e80 4 q320 4 th 4 xa 4 cc 4 kk 64 "
                "f1 64 f2 32 f3 16 yb0 256 yb1 256",
-    "int32": "part 4 par 2 low 4 yy 2 yo 2 ew 16 pos 16 num 16 cb 24 pb 24 selk 4",
-    "uint16": "off1 16 off0 16 l1u 32 eu 16 l2u 16 lou 6 flu 16 sel 2 selz 4 rep 4 bl 8",
+    "int32": "part 4 par 2 low 4 yy 2 yo 2 ew 16 pos 16 num 16 k5 2 x20 5 lq 1 selk 6",
+    "uint16": "off1 16 off0 16 l1u 32 eu 16 l2u 16 lou 6 flu 16 sel 2 sel1 2 selh 2 selz 6 rep 4 bl 6 gl 2",
 }
+STEPS = ("low0 rest crt0 l0 low par l4 i4 rep st0 lowf odd rest0 S0 st1 cn0 lq lowa lowb yy selz e4 k5 x20 "
+         "less lqf yo cr ind S1 crt wj cum wn wp z mm zi m2 cn t1 y16 selh t2 x0 pos x1 num sel eu off1 row k19 "
+         "win1 p wt1 p l1u gf bl hop1 "
+         "y05 gl S2 P sel1 eb ta cb tb sf da mx ge dd vl own h1 xa th h3 cc l2 hop2 "
+         "lou o2 w0 w1 kk f1 f2 f3 flu")
 SCRATCH = {"ps": ("psum", [128, 2048], "float32")}
 for _t, _l in BUFFERS.items():
     _w = _l.split()
@@ -55,10 +60,7 @@ def rank_program(g, core, T, topo):
         return
     A, F = AluOpType, ActivationFunctionType
     S = T.sem
-    turn = [(me + 1 + i) % N for i in range(N)]
-    others = turn[:N - 1]
-    at = ORDER.index(me)
-    others2 = [ORDER[(at + 1 + i) % N] for i in range(N - 1)]
+    others = [(me + 1 + i) % N for i in range(N - 1)]
     mine = plan(core, T.cores, topo)
     arrive = sum(len(plan(T.cores[r], T.cores, topo)[core]) for r in others)
     leave = sum(len(e) for e in mine.values())
@@ -113,9 +115,9 @@ def rank_program(g, core, T, topo):
         need("v", *named(a, b, offs))
         done("v", v.tensor_tensor(ap(out), via(a, offs), ap(b), op), [out])
 
-    def ts(out, a, s1, op, s2=None, op2=None):
-        need("v", *named(a, s1, s2))
-        a, s1, s2 = ap(a), val(s1), val(s2)
+    def ts(out, a, s1, op, s2=None, op2=None, offs=None):
+        need("v", *named(a, s1, s2, offs))
+        a, s1, s2 = via(a, offs), val(s1), val(s2)
         done("v", v.tensor_scalar(ap(out), a, s1, s2, op, op2) if op2 else v.tensor_scalar(ap(out), a, s1, None, op), [out])
 
     def tr(out, i):
@@ -127,6 +129,7 @@ def rank_program(g, core, T, topo):
         done("v", v.tensor_tensor_scan(ap(out), ap(a), ap(b), val(initial), op0, op1), [out])
 
     def fill(x, c):
+        need("v", name(x))
         done("v", v.memset(ap(x), c), [x])
 
     def iota(out, pat, base=0, cm=0, whole=False):
@@ -173,139 +176,182 @@ def rank_program(g, core, T, topo):
     load("y", "wb", T.w[:, :], "ld_w")
 
     iota("part", [[0, 4]], 0, 1, True)
-    iota("cls", [[1, N], [0, 16]], int(RND))
-    iota("selk", [[64, 2], [16, 2]], 15, 0, True)
-    iota("cjk", [[N * LC, 2], [16, 4]], -2)
+    iota("thr", [[COLS, N - 1], [0, 16]], COLS)
+    iota("k16", [[1, 16]])
+    for i, c in enumerate((15, 31, 79)):
+        iota(("selk", i, 6, 3), [[32, 2]], c, 0, True)
+    iota("c16", [[16, 5]])
     iota("partf", [[0, 1]], 0, 1)
     iota("idt", [[1, W1]])
     iota("tab", [[ST, N], [1, PK1]], -int(MID))
-    iota("e8", [[8 * PK1 + N * UP8, 5], [UP8, N]])
-    iota("twi", [[-PK1, 4], [0, N], [16, LC]], -PK1)
-    fill("low0", -NONE)
-    fill("restart", -NONE)
-    fill("crt", 0.0)
-    ts("par", ("part", 0, 2), 4, A.logical_shift_right, 1, A.bitwise_and)
-    ts("low", "part", 15, A.bitwise_and)
-    cp("odd", "par")
-    fill(("restart", 0, 64, 16), 0.0)
-    cp("lowf", ("low", 0, 1))
-    cp("rep", "low")
-    ts(("low0", 16, 17), ("par", 0, 1), -(COLS - 1.0), A.mult)
-    fill(("cn", 0, 1), 0.0)
-    cp("selz", "selk")
-    odd = ("odd", 0, 1)
-    act("odd16", odd, scale=16.0)
-    act("sh1", "lowf", scale=8.0, bias=float(A2))
-    act("sh2", odd, scale=144.0, bias="sh1")
-    act("shift", "partf", scale=-8.0, bias="sh2")
-    tt("yy", ("low", 0, 2), "par", A.subtract)
-    fill(("cb", 0, 8), 0)
-    ts("yo", "yy", 1, A.bitwise_and)
-    ts("y16", ("yy", 0, 1), 16.0, A.mult)
-    fill(("pb", 0, 8), 0)
-    ts("sel", "yo", 32.0, A.mult, "y16", A.add)
-    ts("bl", "cjk", "lowf", A.add, 0.2, A.mult)
 
-    ts("ec", "ew", 1.0 / COLS, A.mult, RND - 0.498, A.add)
-    tt("ind", "ec", "cls", A.is_equal, "rep")
-    scan("cr", "restart", "ind", 0.0, A.min, A.add)
-    act("indc", "ind", scale=COLS + 1.0)
-    for u in (0, 1):
-        tr(("crt", 64 * u, 64 * u + 32), ("cr", 32 * u, 32 * u + 32))
-    scan(("cum", 0, 80), ("low0", 0, 80), ("crt", 0, 80), ("low0", 16, 17), A.min, A.add)
-    scan(("cum", 80, 128), ("low0", 80, 128), ("crt", 80, 128), ("cum", 63, 64), A.min, A.add)
-    tr("z", "cum")
-    tt("pp", "z", "cr", A.subtract, "selz")
-    ts(("cn", 1, 3), ("z", 47, 112, 64), 0.25, A.mult)
-    ts(("cn", 3, 4), ("z", 63, 64), -0.25, A.mult, 0.25, A.add)
-    mine4 = ("cland", 4 * me, 4 * me + 4)
-    need("y", "cn")
-    load("y", mine4, T.cn[:], "cnt")
-    send("cnt", "cn", mine4, lambda d: (0, 4))
-    tt("pm", "pp", "indc", A.mult)
-    ts("eu", "ew", "shift", A.add)
-    tt("pm2", ("pm", 0, 32), ("pm", 32, 64), A.add)
-    tt("pos", ("pm2", 0, 16), ("pm2", 16, 32), A.subtract)
-    ts("num", "pos", 2, A.logical_shift_right, COLS - 1, A.bitwise_and)
-    ts("off1", "num", "odd16", A.add)
-    cp("off0", "num")
-    act("win1", "idt", scale=0.0)
-    act("ebs", "e8", scale=0.125)
-    act("ttw", "twi", bias="lowf")
-    act("prow", "tab", "off0")
-    act(("win2", A2, A2 + W1), "idt", scale=0.0, bias=NONE)
-    for x in (("dd", 0, 4), ("dd", 16, 20), ("sf", 16, 20), ("cland", 16, 20)):
-        act(x, ("idt", 0, 4), scale=0.0)
-
-    scatter("win1", "off1", ("idt", 0, COLS))
-    quant("x", 0, H)
-    tr("wt1", "win1")
-    quant("x", H, COLS)
-    cp("l1u", "wt1", "sel")
+    odd, half = ("odd", 0, 1), ("selh", 0, 1)
     a1, b1 = PK1 * me, PK1 * (me + 1)
     mix, own = ("l1u", 4 * me + 4, 4 * me + 16), ("l1u", 4 * me, 4 * me + 4)
-    pick("v", "slot1q", "xq", mix)
-    pick("s", "slot1s", "xs", mix)
-    pick("s", ("land1s", a1, b1), "xs", own)
-    cut1 = lambda d: (PK1 * others.index(d), PK1 * (others.index(d) + 1))
-    send("p1c", "slot1q", ("land1q", a1, b1), cut1, True)
-    send("p1s", "slot1s", ("land1s", a1, b1), cut1)
+    mine4, mine16 = ("cland", 4 * me, 4 * me + 4), (16 * me, 16 * me + 16)
+    own2, pk2 = (ST * me, ST * me + ST), (ST * me, ST * me + PK2)
+    pieces = [0]
 
-    scatter("win2", "eu", "prow")
+    def columns():
+        act("c15", "lowf", scale=-16.0, bias=-15.0)
+        act("odd16", odd, scale=16.0)
+        act("odd8", odd, scale=8.0)
+        act(("cr", 48, 64), "k16", bias="c15")
+        act("sh1", "lowf", scale=8.0, bias=float(A2 + 16))
+        act("sh2", odd, scale=128.0, bias="sh1")
+        act("shift", "partf", scale=-8.0, bias="sh2")
 
-    act("aa", ("cland", 0, 16), bias=RND + (N - 1 - me) / 4.0 - 0.375)
-    tt("eb", ("cland", 0, 17), ("ebs", 0, 17), A.add)
-    tr("wt2", ("win2", A2, A2 + W1))
-    tt(("cb", 8, 24), ("eb", 1, 17), ("eb", 0, 16), A.subtract)
-    mine16 = (16 * me, 16 * me + 16)
-    cp(("vland",) + mine16, "wt2", ("sel", 0, 1))
-    send("plc", "vland", ("vland",) + mine16, lambda d: mine16)
-    tt("da", ("aa", 4, 16), ("aa", 0, 12), A.subtract)
-    tt(("pb", 8, 24), ("cb", 4, 20), ("cb", 0, 16), A.add)
-    tt(("dd", 4, 16), "da", ("cb", 8, 20), A.subtract)
-    tt(("sf", 0, 16), ("pb", 8, 24), ("pb", 0, 16), A.add)
-    tt(("h1", 0, 32), "aa", ("ttw", 0, 32), A.add, ("bl", 0, 2))
-    tt("ge", "sf", ("ttw", 0, 64), A.is_le, ("bl", 4, 8))
-    pick("v", ("land1q", a1, b1), "xq", own)
-    tt(("h1", 20, 84), "dd", "ge", A.mult, ("bl", 4, 8))
-    tt("h2", ("h1", 0, 40), ("h1", 40, 80), A.add)
-    tt("h3", ("h2", 0, 20), ("h2", 20, 40), A.add)
+    def fills():
+        act(("wt", 48, 96), ("ind", 16, 64), scale=COLS + 1.0)
+        act("msk", ("idt", 0, 20), scale=0.0, bias=1.0)
+        act("win1", "idt", scale=0.0)
+        act(("win2", A2, A2 + W1), "idt", scale=0.0, bias=NONE)
+        need("s", "win1")
+        act(("msk", 0, 20, 5), ("idt", 0, 4), scale=0.0)
+        for x in (("dd", 0, 1), ("sf", 0, 1), ("cland", 16, 17)):
+            act(x, ("idt", 0, 1), scale=0.0)
+
+    def counts():
+        ts(("cn", 1, 3), ("z", 47, 64, 16), 0.25, A.mult)
+        ts(("cn", 3, 4), ("z", 111, 112), 0.25, A.mult)
+        need("y", "cn")
+        load("y", mine4, T.cn[:], "cnt")
+        send("cnt", "cn", mine4, lambda d: (0, 4))
+        iota("qi", [[1, 7], [0, 5]])
+        iota("twi", [[0, N], [16, LC], [RUP, N]])
+        iota("d0i", [[0, N], [16, LC], [4096, N]])
+
+    def row():
+        cp("off0", "num", half)
+        act("prow", "tab", ("off0", 0, 8))
+        act("ebs", "qi", scale=RUP + 0.375)
+        act("ttw", "twi", bias="lowf")
+        act("d0", "d0i", bias="lowf")
+        need("s", "ebs")
+        act(("ebs", 0, 35, 5), ("qi", 0, 7), scale=0.0)
+        act(("ebs", 21, 25), ("qi", 21, 25), scale=RUP + 0.375, bias=COLS / 4)
+
+    def piece(n=1):
+        k = pieces[0]
+        pieces[0] += n
+        scatter("win2", ("eu", 2 * k, 2 * (k + n)), ("prow", 32 * k, 32 * (k + n)))
+
+    def hop1():
+        pick("v", "slot1q", "xq", mix)
+        pick("s", "slot1s", "xs", mix)
+        pick("s", ("land1s", a1, b1), "xs", own)
+        cut1 = lambda d: (PK1 * others.index(d), PK1 * (others.index(d) + 1))
+        send("p1c", "slot1q", ("land1q", a1, b1), cut1, True)
+        send("p1s", "slot1s", ("land1s", a1, b1), cut1)
+
+    def bases():
+        act("aa", ("cland", 0, 17), "gl", bias=RND + (N - 1 - me) / 4.0 - 0.375)
+        act("aa2", ("aa", 0, 20), bias=float(RUP + PK1))
+        base = ("cland", me, 16, 4)
+        act("aq", base, bias=RND - 0.375)
+        act("e80", base, scale=4.0 * ST, bias=-MID - 0.5)
+        act("q320", "aq", scale=4.0 * ST, bias=-4.0 * ST * RND)
+
+    def places():
+        cp(("vland",) + mine16, "mx", ("sel1", 0, 1))
+        send("plc", "vland", ("vland",) + mine16, lambda d: mine16)
 
     def cut(out, a, b):
-        ts(out, ("h3", a, b), PK1 - RND, A.add, float(COLS - 1), A.min)
-    after = LC * (N - 1 - at)
-    if after:
-        cut(("l2u", 0, after), LC * (at + 1), LC * N)
-    if at:
-        cut(("l2u", after, after + LC * at), 0, LC * at)
-    base = ("cland", at, 16, 4)
-    act("aq", base, bias=RND - 0.375)
-    act("e64", base, scale=4.0 * ST, bias=-MID - 0.5)
-    act("q256", "aq", scale=4.0 * ST, bias=-4.0 * ST * RND)
+        ts(out, ("h3", 4 * a + 3, 4 * b, 4), -float(RUP + PK1), A.add, float(COLS - 1), A.min)
 
-    own2 = (ST * me, ST * me + ST)
-    pk2 = (ST * me, ST * me + PK2)
-    pick("v", "slot2q", "land1q", ("l2u", 0, 3 * LC))
-    cut(("lou", 0, LC), LC * at, LC * at + LC)
-    tt("xa", ("sf", at, 16, 4), "aq", A.subtract)
-    pick("v", ("land2q",) + own2, "land1q", ("lou", 0, LC))
-    pick("s", "slot2s", "land1s", ("l2u", 0, 3 * LC))
-    pick("s", ("land2s",) + own2, "land1s", ("lou", 0, LC))
-    cut2 = lambda d: (ST * others2.index(d), ST * others2.index(d) + PK2)
-    send("p2c", "slot2q", ("land2q",) + pk2, cut2, True)
-    send("p2s", "slot2s", ("land2s",) + pk2, cut2)
+    def list2():
+        after = LC * (N - 1 - me)
+        if after:
+            cut(("l2u", 0, after), LC * (me + 1), LC * N)
+        if me:
+            cut(("l2u", after, after + LC * me), 0, LC * me)
 
-    tt("th", "e64", "q256", A.subtract)
-    tt("cc", "xa", ("idt", 0, COLS, PK1), A.add)
-    quant("w", 0, COLS)
-    for r in range(N):
-        ts(("kk", 16 * r, 16 * r + 16), ("vland", 16 * r, 16 * r + 16), ("th", r, r + 1), A.is_ge, ("cc", r, r + 1), A.add)
-    tt("f1", "vland", "kk", A.add)
-    tt("f2", ("f1", 0, 32), ("f1", 32, 64), A.max)
-    tt("f3", ("f2", 0, 16), ("f2", 16, 32), A.max)
-    need("v", "f3")
-    for p in range(0, 128, 32):
-        done("v", v.tensor_scalar(T.flu[p:p + 32, :], T.f3[32 * me:32 * me + 32, :], RND + MID - 1, None, A.add), ["flu"])
+    def hop2():
+        pick("v", "slot2q", "land1q", ("l2u", 0, 3 * LC))
+        pick("s", "slot2s", "land1s", ("l2u", 0, 3 * LC))
+        cut2 = lambda d: (ST * others.index(d), ST * others.index(d) + PK2)
+        send("p2c", "slot2q", ("land2q",) + pk2, cut2, True)
+        send("p2s", "slot2s", ("land2s",) + pk2, cut2)
+
+    def adjust():
+        for r in range(N):
+            ts(("kk", 16 * r, 16 * r + 16), ("vland", 16 * r, 16 * r + 16), ("th", r, r + 1), A.is_ge, ("cc", r, r + 1), A.add)
+
+    def spread():
+        need("v", "f3")
+        for p in range(0, 128, 32):
+            done("v", v.tensor_scalar(T.flu[p:p + 32, :], T.f3[32 * me:32 * me + 32, :], RND + MID - 1, None, A.add), ["flu"])
+
+    step = {
+        "low0": lambda: fill("low0", -NONE), "rest": lambda: fill("restart", -NONE), "crt0": lambda: fill("crt", 0.0),
+        "rest0": lambda: fill(("restart", 0, 48, 16), 0.0),
+        "cn0": lambda: fill(("cn", 0, 1), 0.0),
+        "lq": lambda: ts("lq", ("low", 0, 1), 3, A.bitwise_and), "lqf": lambda: ts("lqf", "lq", 1.0, A.add),
+        "lowa": lambda: ts("lowa", ("low", 0, 1), 0.2, A.mult, -0.4, A.add),
+        "lowb": lambda: ts("lowb", ("low", 0, 1), 0.05, A.mult, -0.475, A.add),
+        "k5": lambda: ts("k5", ("c16", 0, 2), 0.2, A.mult, "lowa", A.add),
+        "x20": lambda: ts("x20", "c16", 0.05, A.mult, "lowb", A.add),
+        "e4": lambda: ts("e4", ("c16", 0, 2), "lowf", A.add, 4.0, A.mult),
+        "k19": lambda: ts("k19", "k5", -19.0, A.mult, -4.0, A.add),
+        "gf": lambda: tt("gf", "e4", "k19", A.add),
+        "gl": lambda: ts("gl", "gf", 16.0, A.min),
+        "par": lambda: ts("par", ("part", 0, 2), 4, A.logical_shift_right, 1, A.bitwise_and),
+        "low": lambda: ts("low", "part", 15, A.bitwise_and),
+        "odd": lambda: cp("odd", "par"), "lowf": lambda: cp("lowf", ("low", 0, 1)), "rep": lambda: cp("rep", "low"),
+        "st0": lambda: fill(("low0", 0, 128, 64), 0.0), "st1": lambda: fill(("low0", 16, 128, 64), 0.0),
+        "l0": lambda: fill(("less", 0, 16), 0.0), "l4": lambda: fill(("less", 64, 80), 1.0), "i4": lambda: fill(("ind", 64, 80), 0.0),
+        "selz": lambda: cp("selz", "selk"), "S0": columns, "S1": fills, "S2": bases,
+        "yy": lambda: tt("yy", ("low", 0, 2), "par", A.subtract), "yo": lambda: ts("yo", "yy", 1, A.bitwise_and),
+        "y16": lambda: ts("y16", ("yy", 0, 1), 16.0, A.mult), "y05": lambda: ts("y05", ("yy", 0, 1), 0.5, A.mult),
+        "sel": lambda: ts("sel", "yo", 32.0, A.mult, "y16", A.add),
+        "sel1": lambda: ts(("sel1", 0, 1), ("yo", 0, 1), 8.5, A.mult, "y05", A.add),
+        "selh": lambda: ts(half, ("low", 0, 1), "odd8", A.add, 15.0, A.min),
+        "bl": lambda: ts(("bl", 0, 5), "x20", 5.0, A.mult, "lqf", A.add),
+        "less": lambda: tt(("less", 16, 64), "ew", "thr", A.is_lt, ("rep", 0, 3)),
+        "ind": lambda: tt(("ind", 0, 64), ("less", 16, 80), ("less", 0, 64), A.subtract),
+        "wj": lambda: tt("wj", ("ind", 16, 80), ("ind", 0, 64), A.subtract),
+        "wp": lambda: ts(("wt", 0, 48), ("wj", 0, 48), -(COLS + 1.0), A.mult),
+        "wn": lambda: ts("wn", "cr", COLS + 1.0, A.mult),
+        "mm": lambda: tt("mm", "wn", "wj", A.mult),
+        "m2": lambda: tt(("zi", 96, 128), ("mm", 0, 32), ("mm", 32, 64), A.add),
+        "cr": lambda: scan(("cr", 0, 48), "restart", ("less", 16, 64), 0.0, A.min, A.add),
+        "crt": lambda: [tr(("crt", 64 * u, 64 * u + 32), ("cr", 32 * u, 32 * u + 32)) for u in (0, 1)],
+        "cum": lambda: scan("cum", "low0", "crt", 0.0, A.min, A.add),
+        "z": lambda: tr("z", "cum"),
+        "zi": lambda: tt(("zi", 0, 96), "z", "wt", A.mult, "selz"), "cn": counts,
+        "t1": lambda: tt("t1", ("zi", 0, 64), ("zi", 64, 128), A.add),
+        "t2": lambda: tt("t2", ("t1", 0, 32), ("t1", 32, 64), A.add),
+        "pos": lambda: tt("pos", ("t2", 0, 16), ("t2", 16, 32), A.add),
+        "num": lambda: ts("num", "pos", 2, A.logical_shift_right, COLS - 1, A.bitwise_and),
+        "off1": lambda: ts("off1", "num", "odd16", A.add),
+        "win1": lambda: scatter("win1", "off1", ("idt", 0, COLS)),
+        "wt1": lambda: tr("wt1", "win1"), "l1u": lambda: cp("l1u", "wt1", "sel"), "hop1": hop1,
+        "x0": lambda: quant("x", 0, H), "x1": lambda: quant("x", H, COLS),
+        "w0": lambda: quant("w", 0, H), "w1": lambda: quant("w", H, COLS),
+        "own": lambda: pick("v", ("land1q", a1, b1), "xq", own),
+        "eu": lambda: ts("eu", "ew", "shift", A.add, offs=half), "row": row, "p": piece, "P": lambda: piece(2),
+        "ta": lambda: tr(("wt2", 0, COLS), ("win2", A2 + 16, A2 + 16 + COLS)),
+        "tb": lambda: tr(("wt2", COLS, COLS + W1), ("win2", A2, A2 + W1)),
+        "mx": lambda: tt("mx", ("wt2", 0, COLS + W1, 32), ("wt2", 16, COLS + W1, 32), A.max), "vl": places,
+        "eb": lambda: tt("eb", ("cland", 0, 17), ("ebs", 0, 32), A.add, "gl"),
+        "cb": lambda: tt("cb", ("eb", 5, 25), ("eb", 0, 20), A.subtract),
+        "da": lambda: tt(("da", 1, 20), ("aa2", 1, 20), ("aa", 0, 19), A.subtract),
+        "dd": lambda: tt(("dd", 1, 20), ("da", 1, 20), ("cb", 0, 19), A.subtract),
+        "sf": lambda: scan(("sf", 1, 20), ("cb", 0, 19), ("msk", 0, 19), 0.0, A.add, A.mult),
+        "ge": lambda: tt("ge", "sf", "ttw", A.is_le, ("bl", 0, 5)),
+        "h1": lambda: tt("h1", "dd", "ge", A.mult, ("bl", 0, 5)),
+        "h3": lambda: scan("h3", "d0", "h1", -NONE, A.min, A.add),
+        "l2": list2, "lou": lambda: cut(("lou", 0, LC), LC * me, LC * me + LC), "hop2": hop2,
+        "o2": lambda: [pick(q, ("land2" + x,) + own2, "land1" + x, ("lou", 0, LC)) for q, x in ("vq", "ss")],
+        "xa": lambda: tt("xa", ("sf", 5 * me + 1, 5 * me + 5), "aq", A.subtract),
+        "th": lambda: tt("th", "e80", "q320", A.subtract),
+        "cc": lambda: tt("cc", "xa", ("twi", 0, N), A.subtract),
+        "kk": adjust, "f1": lambda: tt("f1", "vland", "kk", A.add),
+        "f2": lambda: tt("f2", ("f1", 0, 32), ("f1", 32, 64), A.max),
+        "f3": lambda: tt("f3", ("f2", 0, 16), ("f2", 16, 32), A.max), "flu": spread,
+    }
+    for k in STEPS.split():
+        step[k]()
 
     for h in (0, 1):
         pick("v", "finq%d" % h, "land2q", ("flu", 8 * h, 8 * h + 8))

from concourse.bass import DstId, RemoteDMATransfer
from concourse.mybir import dt, AluOpType, ActivationFunctionType

N, COLS, O = 4, 256, 2
H = COLS // 2
PK1 = COLS // N
PK2 = COLS // N + N - 1
ST = 80
LC = ST // 16
W1 = COLS + 32
A2 = (N - 1) * COLS
NONE = -8192.0
RND = 160.0
MID = 128.0
RUP = 128
BUFFERS = {
    "float8_e4m3fn_x4": "xq 256 wq 256 slot1q 192 land1q 256 slot2q 240 land2q 320 finq0 128 finq1 128",
    "uint8": "xs 256 ws 256 slot1s 192 land1s 256 slot2s 240 land2s 320 fins0 128 fins1 128",
    "bfloat16": "xb 1024 wb 1024 restart 48 low0 128 less 80 ind 80 wj 64 cr 64 crt 128 cum 128 z 128 "
                "win1 288 wt1 288 tab 256 prow 128 win2 1808 wt2 544 mx 17 vland 64 cn 4 cland 24 aa 32 aq 4 cb 20 msk 20",
    "float32": "idt 288 partf 1 odd 2 lowf 1 y16 1 y05 1 odd8 1 odd16 1 sh1 1 sh2 1 shift 1 c16 5 qi 35 ebs 35 twi 80 ttw 80 "
               "d0i 80 d0 80 lowa 1 lowb 1 lqf 1 e4 2 k19 2 gf 2 aa2 20 thr 48 k16 16 c15 1 wt 96 wn 64 mm 64 zi 128 t1 64 t2 32 "
               "eb 32 sf 20 da 20 dd 20 ge 80 h1 80 h3 80 e80 4 q320 4 th 4 xa 4 cc 4 kk 64 "
               "f1 64 f2 32 f3 16 yb0 256 yb1 256",
    "int32": "part 4 par 2 low 4 yy 2 yo 2 ew 16 pos 16 num 16 k5 2 x20 5 lq 1 selk 6",
    "uint16": "off1 16 off0 16 l1u 32 eu 16 l2u 16 lou 6 flu 16 sel 2 sel1 2 selh 2 selz 6 rep 4 bl 6 gl 2",
}
STEPS = ("low0 rest crt0 l0 low par l4 i4 rep st0 lowf odd rest0 S0 st1 cn0 lq lowa lowb yy selz e4 k5 x20 "
         "less lqf yo cr ind S1 crt wj cum wn wp z mm zi m2 cn t1 y16 selh t2 x0 pos x1 num sel eu off1 row k19 "
         "win1 p wt1 p l1u gf bl hop1 "
         "y05 gl S2 P sel1 eb ta cb tb sf da mx ge dd vl own h1 xa th h3 cc l2 hop2 "
         "lou o2 w0 w1 kk f1 f2 f3 flu")
SCRATCH = {"ps": ("psum", [128, 2048], "float32")}
for _t, _l in BUFFERS.items():
    _w = _l.split()
    for _n, _c in zip(_w[0::2], _w[1::2]):
        SCRATCH[_n] = ("sbuf", [128, int(_c)], _t)
SEMAPHORES = "sv sa sg st ld_e ld_x ld_w cnt p1c p1s plc p2c p2s sent out".split()


def plan(src, cores, topo):
    near = set(topo.cores_of(src))
    far = [d for d in cores if d not in near]
    close = [d for d in cores if d in near and d != src]
    out, used = {}, set()
    for group in (far, close):
        if group:
            eng = [e for e in topo.engines(src, group[0]) if e not in used]
            per = len(eng) // len(group)
            for i, d in enumerate(group):
                out[d] = eng[per * i:per * (i + 1)]
            used.update(eng)
    least = min(len(e) for e in out.values())
    return {d: e[::len(e) // least] for d, e in out.items()}


def rank_program(g, core, T, topo):
    me = T.rank_of(core)
    if me is None:
        return
    A, F = AluOpType, ActivationFunctionType
    S = T.sem
    others = [(me + 1 + i) % N for i in range(N - 1)]
    mine = plan(core, T.cores, topo)
    arrive = sum(len(plan(T.cores[r], T.cores, topo)[core]) for r in others)
    leave = sum(len(e) for e in mine.values())
    v, s, te, sy = g.vector, g.scalar, g.tensor, g.sync
    own_sem = {"v": "sv", "s": "sa", "g": "sg", "t": "st"}
    queue = {"v": v, "s": s, "g": g, "t": te, "y": sy}
    cnt = {k: 0 for k in SEMAPHORES}
    made = {}
    seen = {}

    def hold(q, sem, k):
        if seen.get((q, sem), 0) < k:
            queue[q].wait_ge(S[sem], k)
            seen[q, sem] = k

    def need(q, *names):
        for n in names:
            for sem, k in made.get(n, {}).items():
                hold(q, sem, k)

    def ap(x):
        return T[x][:] if not isinstance(x, tuple) else T[x[0]][:, slice(*x[1:])]

    def name(x):
        return x[0] if isinstance(x, tuple) else x

    def named(*xs):
        return [name(x) for x in xs if isinstance(x, (str, tuple))]

    def val(x):
        return ap(x) if isinstance(x, (str, tuple)) else x

    def via(x, offs):
        return ap(x) if offs is None else ap(x).indirect(ap(offs))

    def done(q, ins, out, sem=None, by=1):
        sem = sem or own_sem[q]
        ins.then_inc(S[sem], by)
        cnt[sem] += by
        for o in out:
            made.setdefault(name(o), {})[sem] = cnt[sem]

    def cp(out, i, offs=None):
        need("v", *named(i, offs))
        done("v", v.tensor_copy(ap(out), via(i, offs)), [out])

    def scatter(win, offs, i):
        need("v", *named(win, offs, i))
        done("v", v.tensor_copy(via(win, offs), ap(i)), [win])

    def tt(out, a, b, op, offs=None):
        need("v", *named(a, b, offs))
        done("v", v.tensor_tensor(ap(out), via(a, offs), ap(b), op), [out])

    def ts(out, a, s1, op, s2=None, op2=None, offs=None):
        need("v", *named(a, s1, s2, offs))
        a, s1, s2 = via(a, offs), val(s1), val(s2)
        done("v", v.tensor_scalar(ap(out), a, s1, s2, op, op2) if op2 else v.tensor_scalar(ap(out), a, s1, None, op), [out])

    def tr(out, i):
        need("v", name(i))
        done("v", v.transpose(ap(out), ap(i)), [out])

    def scan(out, a, b, initial, op0, op1):
        need("v", *named(a, b, initial))
        done("v", v.tensor_tensor_scan(ap(out), ap(a), ap(b), val(initial), op0, op1), [out])

    def fill(x, c):
        need("v", name(x))
        done("v", v.memset(ap(x), c), [x])

    def iota(out, pat, base=0, cm=0, whole=False):
        kw = {} if whole else {"allow_small_or_imprecise_dtypes": True}
        done("g", g.iota(ap(out), pat, base, cm, **kw), [out])

    def act(out, i, offs=None, **kw):
        need("s", *named(i, offs, *kw.values()))
        done("s", s.activation(ap(out), via(i, offs), F.Identity, **{k: val(x) for k, x in kw.items()}), [out])

    def load(q, out, src, sem):
        done(q, queue[q].dma_start(ap(out), src), [out], sem, 16)

    def quant(k, a, b):
        need("v", k + "b")
        done("v", v.quantize_mx(ap((k + "q", a, b)), ap((k + "s", a, b)), ap((k + "b", 4 * a, 4 * b))), [k + "q", k + "s"])

    def pick(q, out, win, offs):
        need(q, win, name(offs))
        if win[-1] == "q":
            done(q, v.tensor_copy(ap(out).bitcast(dt.uint32), ap(win).bitcast(dt.uint32).indirect(ap(offs))), [out])
        elif q == "v":
            done(q, v.tensor_copy(ap(out), via(win, offs)), [out])
        else:
            done(q, s.activation(ap(out), via(win, offs), F.Copy), [out])

    def send(sem, buf, dst, cut, codes=False):
        need("g", buf)
        raw = (lambda t: t.bitcast(dt.uint8)) if codes else (lambda t: t)
        tl = []
        for d in others:
            rid, pid = topo.addr(T.cores[d], core)
            tl.append(RemoteDMATransfer(dst_ids=[DstId(rid=rid, pnc=pid)], dma_engine_mask=sum(1 << e for e in mine[T.cores[d]]),
                                        remote_sem=S[sem], src=raw(ap((buf,) + cut(d))), dst=raw(ap(dst))))
        g.remote_dma_fused(tl, local_sem=S.sent)
        cnt["sent"] += leave
        cnt[sem] += arrive
        made.setdefault(name(dst), {})[sem] = cnt[sem]

    for q, k0 in (("y", 0), ("s", 4)):
        for k in range(k0, k0 + 4):
            done(q, queue[q].dma_start(T.ew[16 * k:16 * k + 16, :], T.to[:, :]), ["ew"], "ld_e", 16)
    load("y", "xb", T.x[:, :], "ld_x")
    load("y", "wb", T.w[:, :], "ld_w")

    iota("part", [[0, 4]], 0, 1, True)
    iota("thr", [[COLS, N - 1], [0, 16]], COLS)
    iota("k16", [[1, 16]])
    for i, c in enumerate((15, 31, 79)):
        iota(("selk", i, 6, 3), [[32, 2]], c, 0, True)
    iota("c16", [[16, 5]])
    iota("partf", [[0, 1]], 0, 1)
    iota("idt", [[1, W1]])
    iota("tab", [[ST, N], [1, PK1]], -int(MID))

    odd, half = ("odd", 0, 1), ("selh", 0, 1)
    a1, b1 = PK1 * me, PK1 * (me + 1)
    mix, own = ("l1u", 4 * me + 4, 4 * me + 16), ("l1u", 4 * me, 4 * me + 4)
    mine4, mine16 = ("cland", 4 * me, 4 * me + 4), (16 * me, 16 * me + 16)
    own2, pk2 = (ST * me, ST * me + ST), (ST * me, ST * me + PK2)
    pieces = [0]

    def columns():
        act("c15", "lowf", scale=-16.0, bias=-15.0)
        act("odd16", odd, scale=16.0)
        act("odd8", odd, scale=8.0)
        act(("cr", 48, 64), "k16", bias="c15")
        act("sh1", "lowf", scale=8.0, bias=float(A2 + 16))
        act("sh2", odd, scale=128.0, bias="sh1")
        act("shift", "partf", scale=-8.0, bias="sh2")

    def fills():
        act(("wt", 48, 96), ("ind", 16, 64), scale=COLS + 1.0)
        act("msk", ("idt", 0, 20), scale=0.0, bias=1.0)
        act("win1", "idt", scale=0.0)
        act(("win2", A2, A2 + W1), "idt", scale=0.0, bias=NONE)
        need("s", "win1")
        act(("msk", 0, 20, 5), ("idt", 0, 4), scale=0.0)
        for x in (("dd", 0, 1), ("sf", 0, 1), ("cland", 16, 17)):
            act(x, ("idt", 0, 1), scale=0.0)

    def counts():
        ts(("cn", 1, 3), ("z", 47, 64, 16), 0.25, A.mult)
        ts(("cn", 3, 4), ("z", 111, 112), 0.25, A.mult)
        need("y", "cn")
        load("y", mine4, T.cn[:], "cnt")
        send("cnt", "cn", mine4, lambda d: (0, 4))
        iota("qi", [[1, 7], [0, 5]])
        iota("twi", [[0, N], [16, LC], [RUP, N]])
        iota("d0i", [[0, N], [16, LC], [4096, N]])

    def row():
        cp("off0", "num", half)
        act("prow", "tab", ("off0", 0, 8))
        act("ebs", "qi", scale=RUP + 0.375)
        act("ttw", "twi", bias="lowf")
        act("d0", "d0i", bias="lowf")
        need("s", "ebs")
        act(("ebs", 0, 35, 5), ("qi", 0, 7), scale=0.0)
        act(("ebs", 21, 25), ("qi", 21, 25), scale=RUP + 0.375, bias=COLS / 4)

    def piece(n=1):
        k = pieces[0]
        pieces[0] += n
        scatter("win2", ("eu", 2 * k, 2 * (k + n)), ("prow", 32 * k, 32 * (k + n)))

    def hop1():
        pick("v", "slot1q", "xq", mix)
        pick("s", "slot1s", "xs", mix)
        pick("s", ("land1s", a1, b1), "xs", own)
        cut1 = lambda d: (PK1 * others.index(d), PK1 * (others.index(d) + 1))
        send("p1c", "slot1q", ("land1q", a1, b1), cut1, True)
        send("p1s", "slot1s", ("land1s", a1, b1), cut1)

    def bases():
        act("aa", ("cland", 0, 17), "gl", bias=RND + (N - 1 - me) / 4.0 - 0.375)
        act("aa2", ("aa", 0, 20), bias=float(RUP + PK1))
        base = ("cland", me, 16, 4)
        act("aq", base, bias=RND - 0.375)
        act("e80", base, scale=4.0 * ST, bias=-MID - 0.5)
        act("q320", "aq", scale=4.0 * ST, bias=-4.0 * ST * RND)

    def places():
        cp(("vland",) + mine16, "mx", ("sel1", 0, 1))
        send("plc", "vland", ("vland",) + mine16, lambda d: mine16)

    def cut(out, a, b):
        ts(out, ("h3", 4 * a + 3, 4 * b, 4), -float(RUP + PK1), A.add, float(COLS - 1), A.min)

    def list2():
        after = LC * (N - 1 - me)
        if after:
            cut(("l2u", 0, after), LC * (me + 1), LC * N)
        if me:
            cut(("l2u", after, after + LC * me), 0, LC * me)

    def hop2():
        pick("v", "slot2q", "land1q", ("l2u", 0, 3 * LC))
        pick("s", "slot2s", "land1s", ("l2u", 0, 3 * LC))
        cut2 = lambda d: (ST * others.index(d), ST * others.index(d) + PK2)
        send("p2c", "slot2q", ("land2q",) + pk2, cut2, True)
        send("p2s", "slot2s", ("land2s",) + pk2, cut2)

    def adjust():
        for r in range(N):
            ts(("kk", 16 * r, 16 * r + 16), ("vland", 16 * r, 16 * r + 16), ("th", r, r + 1), A.is_ge, ("cc", r, r + 1), A.add)

    def spread():
        need("v", "f3")
        for p in range(0, 128, 32):
            done("v", v.tensor_scalar(T.flu[p:p + 32, :], T.f3[32 * me:32 * me + 32, :], RND + MID - 1, None, A.add), ["flu"])

    step = {
        "low0": lambda: fill("low0", -NONE), "rest": lambda: fill("restart", -NONE), "crt0": lambda: fill("crt", 0.0),
        "rest0": lambda: fill(("restart", 0, 48, 16), 0.0),
        "cn0": lambda: fill(("cn", 0, 1), 0.0),
        "lq": lambda: ts("lq", ("low", 0, 1), 3, A.bitwise_and), "lqf": lambda: ts("lqf", "lq", 1.0, A.add),
        "lowa": lambda: ts("lowa", ("low", 0, 1), 0.2, A.mult, -0.4, A.add),
        "lowb": lambda: ts("lowb", ("low", 0, 1), 0.05, A.mult, -0.475, A.add),
        "k5": lambda: ts("k5", ("c16", 0, 2), 0.2, A.mult, "lowa", A.add),
        "x20": lambda: ts("x20", "c16", 0.05, A.mult, "lowb", A.add),
        "e4": lambda: ts("e4", ("c16", 0, 2), "lowf", A.add, 4.0, A.mult),
        "k19": lambda: ts("k19", "k5", -19.0, A.mult, -4.0, A.add),
        "gf": lambda: tt("gf", "e4", "k19", A.add),
        "gl": lambda: ts("gl", "gf", 16.0, A.min),
        "par": lambda: ts("par", ("part", 0, 2), 4, A.logical_shift_right, 1, A.bitwise_and),
        "low": lambda: ts("low", "part", 15, A.bitwise_and),
        "odd": lambda: cp("odd", "par"), "lowf": lambda: cp("lowf", ("low", 0, 1)), "rep": lambda: cp("rep", "low"),
        "st0": lambda: fill(("low0", 0, 128, 64), 0.0), "st1": lambda: fill(("low0", 16, 128, 64), 0.0),
        "l0": lambda: fill(("less", 0, 16), 0.0), "l4": lambda: fill(("less", 64, 80), 1.0), "i4": lambda: fill(("ind", 64, 80), 0.0),
        "selz": lambda: cp("selz", "selk"), "S0": columns, "S1": fills, "S2": bases,
        "yy": lambda: tt("yy", ("low", 0, 2), "par", A.subtract), "yo": lambda: ts("yo", "yy", 1, A.bitwise_and),
        "y16": lambda: ts("y16", ("yy", 0, 1), 16.0, A.mult), "y05": lambda: ts("y05", ("yy", 0, 1), 0.5, A.mult),
        "sel": lambda: ts("sel", "yo", 32.0, A.mult, "y16", A.add),
        "sel1": lambda: ts(("sel1", 0, 1), ("yo", 0, 1), 8.5, A.mult, "y05", A.add),
        "selh": lambda: ts(half, ("low", 0, 1), "odd8", A.add, 15.0, A.min),
        "bl": lambda: ts(("bl", 0, 5), "x20", 5.0, A.mult, "lqf", A.add),
        "less": lambda: tt(("less", 16, 64), "ew", "thr", A.is_lt, ("rep", 0, 3)),
        "ind": lambda: tt(("ind", 0, 64), ("less", 16, 80), ("less", 0, 64), A.subtract),
        "wj": lambda: tt("wj", ("ind", 16, 80), ("ind", 0, 64), A.subtract),
        "wp": lambda: ts(("wt", 0, 48), ("wj", 0, 48), -(COLS + 1.0), A.mult),
        "wn": lambda: ts("wn", "cr", COLS + 1.0, A.mult),
        "mm": lambda: tt("mm", "wn", "wj", A.mult),
        "m2": lambda: tt(("zi", 96, 128), ("mm", 0, 32), ("mm", 32, 64), A.add),
        "cr": lambda: scan(("cr", 0, 48), "restart", ("less", 16, 64), 0.0, A.min, A.add),
        "crt": lambda: [tr(("crt", 64 * u, 64 * u + 32), ("cr", 32 * u, 32 * u + 32)) for u in (0, 1)],
        "cum": lambda: scan("cum", "low0", "crt", 0.0, A.min, A.add),
        "z": lambda: tr("z", "cum"),
        "zi": lambda: tt(("zi", 0, 96), "z", "wt", A.mult, "selz"), "cn": counts,
        "t1": lambda: tt("t1", ("zi", 0, 64), ("zi", 64, 128), A.add),
        "t2": lambda: tt("t2", ("t1", 0, 32), ("t1", 32, 64), A.add),
        "pos": lambda: tt("pos", ("t2", 0, 16), ("t2", 16, 32), A.add),
        "num": lambda: ts("num", "pos", 2, A.logical_shift_right, COLS - 1, A.bitwise_and),
        "off1": lambda: ts("off1", "num", "odd16", A.add),
        "win1": lambda: scatter("win1", "off1", ("idt", 0, COLS)),
        "wt1": lambda: tr("wt1", "win1"), "l1u": lambda: cp("l1u", "wt1", "sel"), "hop1": hop1,
        "x0": lambda: quant("x", 0, H), "x1": lambda: quant("x", H, COLS),
        "w0": lambda: quant("w", 0, H), "w1": lambda: quant("w", H, COLS),
        "own": lambda: pick("v", ("land1q", a1, b1), "xq", own),
        "eu": lambda: ts("eu", "ew", "shift", A.add, offs=half), "row": row, "p": piece, "P": lambda: piece(2),
        "ta": lambda: tr(("wt2", 0, COLS), ("win2", A2 + 16, A2 + 16 + COLS)),
        "tb": lambda: tr(("wt2", COLS, COLS + W1), ("win2", A2, A2 + W1)),
        "mx": lambda: tt("mx", ("wt2", 0, COLS + W1, 32), ("wt2", 16, COLS + W1, 32), A.max), "vl": places,
        "eb": lambda: tt("eb", ("cland", 0, 17), ("ebs", 0, 32), A.add, "gl"),
        "cb": lambda: tt("cb", ("eb", 5, 25), ("eb", 0, 20), A.subtract),
        "da": lambda: tt(("da", 1, 20), ("aa2", 1, 20), ("aa", 0, 19), A.subtract),
        "dd": lambda: tt(("dd", 1, 20), ("da", 1, 20), ("cb", 0, 19), A.subtract),
        "sf": lambda: scan(("sf", 1, 20), ("cb", 0, 19), ("msk", 0, 19), 0.0, A.add, A.mult),
        "ge": lambda: tt("ge", "sf", "ttw", A.is_le, ("bl", 0, 5)),
        "h1": lambda: tt("h1", "dd", "ge", A.mult, ("bl", 0, 5)),
        "h3": lambda: scan("h3", "d0", "h1", -NONE, A.min, A.add),
        "l2": list2, "lou": lambda: cut(("lou", 0, LC), LC * me, LC * me + LC), "hop2": hop2,
        "o2": lambda: [pick(q, ("land2" + x,) + own2, "land1" + x, ("lou", 0, LC)) for q, x in ("vq", "ss")],
        "xa": lambda: tt("xa", ("sf", 5 * me + 1, 5 * me + 5), "aq", A.subtract),
        "th": lambda: tt("th", "e80", "q320", A.subtract),
        "cc": lambda: tt("cc", "xa", ("twi", 0, N), A.subtract),
        "kk": adjust, "f1": lambda: tt("f1", "vland", "kk", A.add),
        "f2": lambda: tt("f2", ("f1", 0, 32), ("f1", 32, 64), A.max),
        "f3": lambda: tt("f3", ("f2", 0, 16), ("f2", 16, 32), A.max), "flu": spread,
    }
    for k in STEPS.split():
        step[k]()

    for h in (0, 1):
        pick("v", "finq%d" % h, "land2q", ("flu", 8 * h, 8 * h + 8))
    for h, q in enumerate("sv"):
        pick(q, "fins%d" % h, "land2s", ("flu", 8 * h, 8 * h + 8))
    for o in range(O):
        for h in (0, 1):
            need("t", "finq%d" % h, "fins%d" % h, "wq", "ws")
            p, wc = 512 * (2 * o + h), (128 * o, 128 * o + 128)
            done("t", te.matmul_mx(T.ps[:, p:p + H], ap(("wq",) + wc), ap(("ws",) + wc), ap("finq%d" % h), ap("fins%d" % h),
                                   True, True), ["ps%d" % p])
    for o in range(O):
        for h, q in enumerate("sv"):
            p, y = 512 * (2 * o + h), ("yb%d" % o, H * h, H * h + H)
            need(q, "ps%d" % p)
            done(q, v.tensor_copy(ap(y), T.ps[:, p:p + H]) if q == "v" else s.activation(ap(y), T.ps[:, p:p + H], F.Copy), [y])
    for o, q in enumerate("ys"):
        need(q, "yb%d" % o)
        done(q, queue[q].dma_start(T.y[:, COLS * o:COLS * o + COLS], T["yb%d" % o][:]), ["stored"], "out", 16)
    hold("y", "out", cnt["out"])
    hold("g", "sent", cnt["sent"])
    hold("g", "sg", cnt["sg"])
